import numpy as np, ml_dtypes
CORES = [3,11,19,27,35,43,51,59]
N = 8
import mx_ref
BF = ml_dtypes.bfloat16
def gcols(t, e):
    v = np.concatenate([t.reshape(8, 16, -1, 4), np.zeros((8, 16, 1, 4), BF)], axis=2)
    return np.ascontiguousarray(np.stack([v[g][:, e[g]] for g in range(8)])).reshape(128, -1)
def tile(rs):
    return np.stack(rs, axis=2).reshape(128, -1).astype(BF)
def cut(t, i, w=512):
    return t[:, w * i:w * i + w]
def pick(q, e):
    c = np.concatenate([q[0].reshape(128, -1, 4), np.zeros((128, 1, 4), np.uint8)], axis=1); s = np.concatenate([q[1], np.ones((16, 1), np.uint8)], axis=1)
    return (np.ascontiguousarray(c[:, e].reshape(128, -1)), np.ascontiguousarray(s[:, e]))
def join(*qs):
    return (np.concatenate([q[0] for q in qs], axis=1), np.concatenate([q[1] for q in qs], axis=1))
def put(q, e, v):
    c, s = q[0].reshape(128, -1, 4).copy(), q[1].copy(); c[:, e] = v[0].reshape(128, -1, 4); s[:, e] = v[1]
    return (c.reshape(128, -1), s)
def pk(c, s):
    return (np.ascontiguousarray(c), mx_ref.live(s))
def emit(q):
    return q[0], q[1]
def packed(v, rng):
    q = [mx_ref.quantize(np.ascontiguousarray(v[r])) for r in range(N)]
    return np.stack([a for a, b in q]), np.stack([mx_ref.plane(b, rng) for a, b in q])
def values_of_codes():
    e, c = np.zeros((128, 128, 4), np.float32), np.zeros((128, 2, 4), np.uint8)
    e[np.arange(128), np.arange(128), 0] = 1
    c[:127, :, 0] = np.arange(256).reshape(2, 128).T[:127]
    return mx_ref.matmul(mx_ref.quantize(e.reshape(128, 512).astype(BF)), (c.reshape(128, 8), np.full((16, 2), 127, np.uint8))).T.reshape(-1).astype(np.float64)
CODE_VALUE, SCALE_VALUE = values_of_codes(), 2.0 ** (np.arange(256) - 127.0)
def decode(q):
    return (CODE_VALUE[q[0]].reshape(16, 8, -1, 4) * SCALE_VALUE[q[1]][:, None, :, None] + 0.0).reshape(128, -1).astype(np.float32)
def f(rng, *shape):
    return mx_ref.flush((rng.standard_normal(shape, dtype=np.float32) * np.exp2(rng.integers(-2, 3, shape[:-1] + (1,)))).astype(BF))
def wide(rng, *shape, cols=0):
    v = rng.standard_normal(shape, dtype=np.float32) * np.exp2(rng.integers(-12, 13, shape)).astype(np.float32)
    if cols: v *= np.repeat(np.exp2(rng.integers(-cols, cols + 1, shape[:-2] + (1, shape[-1] // 4))) * (rng.random(shape[:-2] + (1, shape[-1] // 4)) > 0.0625), 4, axis=-1).astype(np.float32)
    return mx_ref.flush(v.astype(BF))
S, C, L, Q1, Q2, R = 256, 192, 64, 14, 52, 3
def numbers_of(rng):
    return {"x": np.array(f(rng, N, 128, 4 * C)), "u": np.array(f(rng, N, 128, 512)), "v": np.array(f(rng, N, 128, 512))}
def weights(rng, w):
    c, p = packed(w, rng)
    return {"wc": c, "ws": p}
def shift(rng, mix=False):
    w = np.zeros((128, 4, 128, 4), np.float32)
    i = np.arange(128)
    first = i[i % 16 < 8]
    i = i[(i % 16 >= 8) & (i % 16 < 14)]
    for b in range(4):
        w[i, b, i, b] = -64
        w[i + 2, b, i, b] = 64
        if mix: w[(first + 16) % 128, b, first, b] = 64
    return weights(rng, np.stack([w.reshape(128, 2048).astype(BF)] * N))
def planned(rng, a, step, k, mix=False):
    d = numbers_of(rng)
    x = d["x"].astype(np.float32).reshape(N, 8, 16, C, 4)
    g = ((a[..., None] >> np.arange(8)) & 1) * 2.0 ** np.arange(8) * step
    x[:, :, 8:] = g.reshape(4, N, 8, C, 2, 4).transpose(1, 2, 0, 4, 3, 5).reshape(N, 8, 8, C, 4)
    u = d["u"].reshape(N, 128, 128, 4)
    u[:, :, ::16] = 0
    for h in range(0, 128, 16): u[:, h + 8:h + 10, h] = k.astype(np.float32).astype(BF)[:, None, None]
    return {"x": d["x"], "u": u.reshape(N, 128, 512), "v": d["v"], **shift(rng, mix)}, x
def with_x(d, x):
    d["x"] = x.astype(np.float32).reshape(N, 128, 4 * C).astype(BF)
    return d
def setup_inputs(rng):
    return {**numbers_of(rng), **weights(rng, f(rng, N, 128, 2048))}
def setup_inputs_ties(rng):
    o = rng.permutation(N)
    a = rng.integers(0, 3, (4, N, 8, C))
    a[:, o[0]] = 1
    d, x = planned(rng, a, 1.0, np.ones(N))
    x[o[1]] = 0
    s = rng.integers(0, 6, (4, 8, C))
    x[o[2], :, 8:] = 0
    for i in range(4):
        x[o[2], :, 8 + 2 * i, :, 0] = (8 + s[i]) * 2.0 ** -33
        x[o[2], :, 9 + 2 * i, :, 0] = (9 + s[i]) * 2.0 ** -33
    u = d["u"].reshape(N, 128, 128, 4)
    for h in range(0, 128, 16):
        u[o[2], h + 8, h] = BF(9 * 2.0 ** -33)
        u[o[2], h + 9, h] = BF(-2.0 ** -30)
    d["u"] = u.reshape(N, 128, 512)
    return with_x(d, x)
def setup_inputs_near(rng):
    k = (np.arange(N) + rng.integers(N)) % N < N // 2
    k = np.where(k, 2.0 ** -30, 1.0)
    d, x = planned(rng, rng.integers(0, 256, (4, N, 8, C)), 2.0 ** -23, k)
    x[:, :, :8] = (0.25 + 0.75 * rng.random((N, 8, 8, C, 4))) * rng.choice([-1.0, 1.0], (N, 8, 8, C, 4))
    x[:, :, 0] = 0
    x[:, :, 0, :, 0] = (rng.permutation(8) % 2 * 2.0 - 1.0)[None, :, None]
    x[k < 1] *= np.float32(2.0 ** -7)
    u = d["u"].reshape(N, 128, 128, 4)
    for h in range(0, 128, 16): u[:, h, h, 0] = k.astype(np.float32).astype(BF)
    d["u"] = u.reshape(N, 128, 512)
    return with_x(d, x)
def setup_inputs_huge(rng):
    d = numbers_of(rng)
    x = 2.0 ** 30 * (0.6 + 0.4 * rng.random((N, 128, C, 4)))
    c = np.stack([rng.permutation(C) % 2 * 2.0 - 1.0 for r in range(N)])
    c[rng.permutation(N) < N // 2] = 1
    x *= c[:, None, :, None]
    u = d["u"].reshape(N, 128, 128, 4)
    s = np.stack([rng.permutation(8) % 2 * 2.0 - 1.0 for r in range(N)])
    u[:, :, ::16] = (2.0 ** 30 * (1 - 0.25 * rng.random((N, 128, 8, 4))) * s[:, None, :, None]).astype(np.float32).astype(BF)
    w = np.zeros((128, 4, 128, 4), np.float32)
    i = np.arange(128)
    for b in range(4): w[i, b, i, b] = 2.0 ** -10
    return with_x({"x": d["x"], "u": u.reshape(N, 128, 512), "v": d["v"], **weights(rng, np.stack([w.reshape(128, 2048).astype(BF)] * N))}, x)
def entering(m, h, rng):
    n = S // 16
    w = np.zeros(n, int)
    rest = L
    if m < 2:
        o = rng.permutation(n // 4)
        w[4 * o[0]:4 * o[0] + 4] = Q1 - h
        rest -= 4 * (Q1 - h)
        for i in o[1:]:
            c = min(rest, Q2 - 4 * h + int(m == 1 and i == o[1]))
            w[4 * i + rng.integers(4)] = c
            rest -= c
    elif m == 2:
        a = int(rng.integers(n))
        w[a] = Q1 + 1 - h
        rest -= Q1 + 1 - h
        for i in rng.permutation(n):
            if i // 4 != a // 4:
                w[i] = min(rest, Q1 - h)
                rest -= w[i]
    elif m == 3: w[rng.integers(n)] = L
    else: w = np.bincount(rng.integers(0, n, L), minlength=n)
    return w
def setup_inputs_crowd(rng):
    n = S // 16
    leaf = np.arange(C) * S // C // 16
    a = rng.integers(0, 256, (4, N, 8, C))
    a[3] = rng.integers(100, 104, (N, 8, C))
    stay = np.ones((N, 8, C), bool)
    m = np.stack([rng.permutation(8) for r in range(N)])
    gone = [[[0], [0, 1], [int(rng.integers(1, n - 2)), n - 1]][i % 3] for i in rng.permutation(N)]
    for r in range(N):
        for g in range(8):
            a[0, r, g] = rng.permutation(C)
            k = np.full(n, L // n)
            if m[r, g] == 6:
                other = np.setdiff1d(np.arange(n), gone[r])
                k[gone[r]] = C // n
                k[rng.permutation(other)] = (L - len(gone[r]) * (C // n) + np.arange(len(other))) // len(other)
            for i in range(n):
                e = rng.permutation(np.flatnonzero(leaf == i))
                if i == 0: e = np.concatenate([[0], e[e > 0]])
                stay[r, g, e[:k[i]]] = False
    for r in range(N):
        for g in range(8):
            if m[r, g] == 4: e = np.zeros(L, int)
            elif m[r, g] == 5: e = np.full(L, C - 1)
            else:
                if m[r, g] == 6:
                    room = Q1 - np.bincount(leaf[stay[r, g]], minlength=n)
                    room[gone[r]] = 0
                    first = np.zeros(6, int)
                    if gone[r][0] > 0:
                        c = gone[r][0] - 1
                        room[[c, n - 2]] -= 2
                        i = int(np.flatnonzero(stay[r, g] & (leaf == c))[-1])
                        first = np.array([i, i, C - 1, C - 1])
                    w = np.bincount(rng.permutation(np.repeat(np.arange(n), room))[:L - len(first)], minlength=n)
                else:
                    w = entering(m[r, g], C // n - L // n, rng)
                    first = np.zeros(L - int(np.sum(w)), int)
                e = np.concatenate([first] + [rng.choice(np.flatnonzero(stay[r, g] & (leaf == i)), w[i]) for i in np.flatnonzero(w)])
            s = (r - 1) % N
            b = rng.integers(C, 256, C)
            b[~stay[s, g][a[0, s, g]]] = rng.permutation(e)
            a[1, s, g] = b
    d, x = planned(rng, a, 1.0, np.ones(N), True)
    return with_x(d, x)
def setup_inputs_spread(rng):
    d = setup_inputs(rng)
    d["x"] = wide(rng, N, 128, 4 * C, cols=6)
    return d
def check_inputs(d):
    b = []
    for k in ("x", "u", "v"):
        a = np.abs(d[k].astype(np.float32))
        if not (np.isfinite(a).all() and ((a == 0) | (a >= 2.0 ** -30) & (a <= 2.0 ** 30)).all()): b.append("a value of " + k)
    for r in range(N):
        if ((d["wc"][r] & 127) == 127).any(): b.append("a code of wc that is no number")
        with np.errstate(over="ignore"): a = np.abs(decode(pk(d["wc"][r], d["ws"][r])))
        if not ((a == 0) | (a >= 2.0 ** -30) & (a <= 2.0 ** 30)).all(): b.append("a value of W (wc, ws)")
    return b
def respread(h, key, new):
    n = np.searchsorted(key[h], new, side="right")
    leaf = np.where(n > 0, h[np.maximum(n - 1, 0)], 0) // 16
    k = np.concatenate([key[h], new])
    i = np.argsort(k, kind="stable")
    src = np.concatenate([h, S + np.arange(L)])[i]
    at = src.copy()
    lf = np.concatenate([h // 16, leaf])[i]
    count = np.bincount(lf, minlength=S // 16)
    size = np.where(count <= Q1, 16, np.where(np.repeat(np.sum(count.reshape(-1, 4), axis=1), 4) <= Q2, 64, S))
    size[np.bincount(leaf, minlength=S // 16) == 0] = 0
    for w in (16, 64, S):
        for s in range(0, S, w):
            if (size[s // 16:(s + w) // 16] == w).any():
                e = np.flatnonzero(lf * 16 // w == s // w)
                at[e] = s + np.arange(len(e)) * w // len(e)
    to, kept = np.full(S, -1), np.zeros(S, np.float32)
    to[at] = src
    kept[at] = k[i]
    return to, kept
def reference(x, u, v, wc, ws):
    qu = [mx_ref.quantize(u[r]) for r in range(N)]
    lay = [pk(wc[r], ws[r]) for r in range(N)]
    start = np.arange(C) * S // C
    now, key, held = [], [], []
    for r in range(N):
        p = mx_ref.matmul(qu[r], mx_ref.quantize(x[r]))[::16] + np.float32(0.0)
        o = np.argsort(p, axis=1, kind="stable")
        e, k = np.full((8, S), -1), np.zeros((8, S), np.float32)
        e[:, start] = o
        k[:, start] = np.take_along_axis(p, o, axis=1)
        now.append(gcols(x[r], e))
        key.append(k)
        held.append(e >= 0)
    y, ol = np.zeros((N, 128, S), np.float32), np.zeros((N, 8, S), np.float32)
    oc, osc = np.zeros((N, 128, 4 * S), np.uint8), np.zeros((N, 16, S), np.uint8)
    for t in range(R):
        made, new, border = [], [], []
        for r in range(N):
            q = mx_ref.quantize(now[r])
            made.append(tile([mx_ref.matmul(pick(lay[r], np.arange(128 * b, 128 * b + 128)), q) * np.float32(0.015625) + now[r][:, b::4].astype(np.float32) for b in range(4)]))
            p = mx_ref.matmul(qu[r], mx_ref.quantize(made[r]))[::16] + np.float32(0.0)
            o = np.argsort(np.where(held[r], p, np.float32(np.inf)), axis=1, kind="stable")[:, :L]
            new.append(np.take_along_axis(p, o, axis=1))
            np.put_along_axis(held[r], o, False, axis=1)
            border.append(mx_ref.quantize(gcols(made[r], o)))
        came = decode(join(*border)).astype(BF)
        for r in range(N):
            e = (r - 1) % N
            to, k = np.full((8, S), -1), np.zeros((8, S), np.float32)
            for g in range(8): to[g], k[g] = respread(np.flatnonzero(held[r][g]), key[r][g], new[e][g])
            now[r] = gcols(np.concatenate([made[r], cut(came, e, 4 * L)], axis=1), to)
            key[r], held[r], ol[r] = k, to >= 0, to
    for r in range(N):
        q = mx_ref.quantize(now[r])
        y[r] = mx_ref.matmul(mx_ref.quantize(v[r]), q)
        oc[r], osc[r] = emit(q)
    return {"y": y, "ol": ol, "oc": oc, "osc": osc}

@@ -1,0 +1,571 @@
+from concourse.mybir import dt, AluOpType, AxisListType, ActivationFunctionType
+
+A = AluOpType
+COPY = ActivationFunctionType.Copy
+IDENT = ActivationFunctionType.Identity
+RELU = ActivationFunctionType.Relu
+SIGN = ActivationFunctionType.Sign
+BIG = 2.0 ** 96
+ROUNDS = 3
+W64 = 4 * 256
+UP_ = 0.5 - 1.0 / 512
+ON_SCALAR = 8
+
+SCRATCH = {}
+
+
+def _decl(names, where, shape, dtype):
+    for n in names.split():
+        SCRATCH[n] = (where, shape, dtype)
+
+
+_decl("XT", "sbuf", [128, 832], "bfloat16")
+_decl("UT VT E0 E1 E2 E3 ONEB", "sbuf", [128, 512], "bfloat16")
+_decl("TI FA FB", "sbuf", [128, 1024], "bfloat16")
+_decl("TP0 TP1 TP2 TP3", "sbuf", [128, 528], "bfloat16")
+_decl("AD0 AD1 AD2 AD3 G0 G1 G2 G3", "sbuf", [128, 256], "bfloat16")
+_decl("CMP", "sbuf", [128, 2304], "bfloat16")
+_decl("JNK", "sbuf", [128, 1536], "bfloat16")
+_decl("CMQ", "sbuf", [128, 768], "float32")
+_decl("CMN", "sbuf", [128, 768], "bfloat16")
+_decl("QX", "sbuf", [128, 192], "float8_e4m3fn_x4")
+_decl("QXS", "sbuf", [128, 192], "uint8")
+_decl("QU QVC UR UP EQ0 EQ1 EQ2 EQ3", "sbuf", [128, 128], "float8_e4m3fn_x4")
+_decl("QUS QVS URS UPS EQS0 EQS1 EQS2 EQS3", "sbuf", [128, 128], "uint8")
+_decl("WQ", "sbuf", [128, 512], "float8_e4m3fn_x4")
+_decl("WS", "sbuf", [128, 512], "uint8")
+_decl("QF QT0 QT1 QT2 LQ0 LQ1 LQ2", "sbuf", [128, 256], "float8_e4m3fn_x4")
+_decl("QFS QTS0 QTS1 QTS2 LS0 LS1 LS2", "sbuf", [128, 256], "uint8")
+_decl("PS0 PS1 PS2 PS3 PP PQ PD0 PD1", "psum", [128, 512], "float32")
+_decl("IOTA HRA HRB", "sbuf", [128, 512], "float32")
+_decl("JM MASK DMASK RST RMIN ONE ZERO TMP TMY TM2 YS PR PPR FLB SFP CSP XWS OLR HROL YO", "sbuf", [128, 256], "float32")
+_decl("KA KB SEQ SEQO", "sbuf", [128, 448], "float32")
+_decl("SEQS XC", "sbuf", [128, 208], "float32")
+_decl("SC Z EQR LROW SF CCS KST KWS XCS LBM LBK", "sbuf", [128, 192], "float32")
+_decl("ARR64", "sbuf", [128, 256], "float32")
+SMALL = ("EB D1 ARB CSMB GM B32 B32T X2 PAR C1C D0A D0B UA UB I0 I1 UX C64I UY C12 RST4 C16 IW C257 M16 M17 CNT RK LFN KWB "
+         "LF3 TB XM XV NCM TH HBP AX BA S4 E64 EQD EP1 CE3 EP3 VL NI ENI EN2 TT JW1 KI0 ENC INV AC0 SP PH LB AR1 S256 HBB HB1 "
+         "S16 S161 CN4 BAD4 ZX4").split()
+_decl("SMALLS", "sbuf", [128, 40 * len(SMALL)], "float32")
+_decl("INTS", "sbuf", [128, 16 * 11], "int32")
+_decl("LW0 LW1 LW2 LP0 LP1 LP2", "sbuf", [128, 4], "uint16")
+_decl("LISTS", "sbuf", [128, 16 * 12], "uint16")
+_decl("OFF", "sbuf", [128, 64], "uint16")
+PIECE = {n: ("SMALLS", 40 * i) for i, n in enumerate(SMALL)}
+PIECE.update({n: ("INTS", 16 * i) for i, n in enumerate("PI SI PHI I2 KI KA4 KB4 UI QI HBI H3".split())})
+PIECE.update({n: ("LISTS", 16 * i) for i, n in enumerate("RKU HUA HUB QVA QVB QDU TU XL AL UL OFY".split())})
+PIECE.update({n: ("ARR64", 64 * i) for i, n in enumerate("LL AOS ARC BIGS".split())})
+
+SEMAPHORES = ["sv", "ss", "st", "sg", "dx", "du", "dw", "dws", "dv", "dout", "loc", "au",
+              "aq0", "aq1", "aq2", "al0", "al1", "al2"]
+
+
+def R(name, a=0, b=16, st=1, off=None, bc=None):
+    n, k = PIECE.get(name, (name, 0))
+    return (n, k + a, k + b, st, off, bc)
+
+
+def rank_program(g, core, T, topo):
+    rank = T.rank_of(core)
+    if rank is None:
+        return
+    nxt = T.cores[(rank + 1) % len(T.cores)]
+
+    Q = {"v": g.vector, "s": g.scalar, "t": g.tensor, "g": g, "y": g.sync}
+    sem_of = {"v": "sv", "s": "ss", "t": "st", "g": "sg"}
+    cnt = {q: 0 for q in Q}
+    known = {q: {} for q in Q}
+    clocks = {}
+    hist = {}
+
+    def ap(r):
+        n, a, b, st, off, bc = r
+        x = T[n][:, a:b] if st == 1 else T[n][:, a:b:st]
+        if bc is not None:
+            x = x.bitcast(bc)
+        if off is not None:
+            x = x.indirect(ap(off))
+        return x
+
+    def meet(h, r):
+        if h[0] >= r[2] or r[1] >= h[1]:
+            return False
+        return not (h[2] > 1 and h[2] == r[3] and (h[0] - r[1]) % h[2])
+
+    def wait(q, src, val):
+        if known[q].get(src, 0) >= val:
+            return
+        Q[q].wait_ge(T.sem[sem_of.get(src, src)], val)
+        for s, v in clocks[(src, val)].items():
+            if known[q].get(s, 0) < v:
+                known[q][s] = v
+
+    def psum(n):
+        return n in SCRATCH and SCRATCH[n][0] == "psum"
+
+    def note(src, val, writes, reads):
+        for w in writes:
+            h = hist.setdefault(w[0], [])
+            if w[3] == 1 and w[4] is None:
+                h[:] = [e for e in h if not (w[1] <= e[0] and e[1] <= w[2])]
+            h.append((w[1], w[2], w[3], True, src, val))
+        for r in reads:
+            hist.setdefault(r[0], []).append((r[1], r[2], r[3], psum(r[0]), src, val))
+
+    def emit(q, call, writes, reads, event=None):
+        reads = list(reads)
+        for r in list(reads) + list(writes):
+            if r[4] is not None:
+                reads.append(r[4])
+        need = {}
+        for r in reads:
+            for h in hist.get(r[0], ()):
+                if meet(h, r) and h[3] and not (psum(r[0]) and h[4] == q):
+                    need[h[4]] = max(need.get(h[4], 0), h[5])
+        for w in writes:
+            for h in hist.get(w[0], ()):
+                if meet(h, w):
+                    need[h[4]] = max(need.get(h[4], 0), h[5])
+        for src in sorted(need, key=lambda s: -len(clocks[(s, need[s])])):
+            wait(q, src, need[src])
+        i = call()
+        if event is None:
+            cnt[q] += 1
+            i.then_inc(T.sem[sem_of[q]], 1)
+            src, val = q, cnt[q]
+        else:
+            src, val, inc = event
+            i.then_inc(T.sem[src], inc)
+        clocks[(src, val)] = dict(known[q])
+        clocks[(src, val)][src] = val
+        note(src, val, writes, reads)
+
+    def lands(src, val, writes):
+        clocks[(src, val)] = {src: val}
+        note(src, val, writes, [])
+
+    def isr(x):
+        return isinstance(x, tuple)
+
+    def val(x):
+        return ap(x) if isr(x) else x
+
+    def tt(o, a, b, op):
+        emit("v", lambda: g.vector.tensor_tensor(ap(o), ap(a), ap(b), op), [o], [a, b])
+
+    def ts(o, a, s1, s2, op0, op1=None):
+        rd = [a] + [x for x in (s1, s2) if isr(x)]
+        if op1 is None:
+            emit("v", lambda: g.vector.tensor_scalar(ap(o), ap(a), val(s1), None, op0), [o], rd)
+        else:
+            emit("v", lambda: g.vector.tensor_scalar(ap(o), ap(a), val(s1), val(s2), op0, op1), [o], rd)
+
+    def cp(o, a):
+        emit("v", lambda: g.vector.tensor_copy(ap(o), ap(a)), [o], [a])
+
+    def scan(o, d0, d1, op0=A.mult, op1=A.add, init=0.0):
+        emit("v", lambda: g.vector.tensor_tensor_scan(ap(o), ap(d0), ap(d1), init, op0, op1), [o], [d0, d1])
+
+    def red(o, a, op):
+        emit("v", lambda: g.vector.tensor_reduce(ap(o), ap(a), AxisListType.X, op), [o], [a])
+
+    def fill(o, c):
+        emit("v", lambda: g.vector.memset(ap(o), c), [o], [])
+
+    def turn(o, a):
+        emit("v", lambda: g.vector.transpose(ap(o), ap(a)), [o], [a])
+
+    def quant(o, s, a, n):
+        o, s, a = R(o, 0, n), R(s, 0, n), R(a, 0, 4 * n)
+        emit("v", lambda: g.vector.quantize_mx(ap(o), ap(s), ap(a)), [o, s], [a])
+
+    def act(o, a, func=COPY, scale=1.0, bias=0.0):
+        rd = [a] + [x for x in (scale, bias) if isr(x)]
+        if func == COPY and not isr(scale) and scale == 1.0:
+            emit("s", lambda: g.scalar.activation(ap(o), ap(a), COPY), [o], rd)
+        elif func == COPY:
+            emit("s", lambda: g.scalar.activation(ap(o), ap(a), COPY, scale=val(scale)), [o], rd)
+        else:
+            emit("s", lambda: g.scalar.activation(ap(o), ap(a), func, bias=val(bias), scale=val(scale)), [o], rd)
+
+    turns = [0]
+
+    def total(o, a, n, func=COPY):
+        j = R("JNK", 192 * (turns[0] % 8), 192 * (turns[0] % 8) + n)
+        turns[0] += 1
+        emit("s", lambda: g.scalar.activation(ap(j), ap(a), func, accum_out=ap(o)), [j, o], [a])
+
+    def mm(o, l, ls, r, rs, n=256, c=0):
+        o, l, ls, r, rs = R(o, 0, n), R(l, c, c + 128), R(ls, c, c + 128), R(r, 0, n), R(rs, 0, n)
+        emit("t", lambda: g.tensor.matmul_mx(ap(o), ap(l), ap(ls), ap(r), ap(rs), True, True), [o], [l, ls, r, rs])
+
+    def iota(o, pattern, base=0, cm=0):
+        if SCRATCH[o[0]][2] == "int32":
+            emit("g", lambda: g.iota(ap(o), pattern, base, cm), [o], [])
+        else:
+            emit("g", lambda: g.iota(ap(o), pattern, base, cm, allow_small_or_imprecise_dtypes=True), [o], [])
+
+    def load(q, o, src, sem):
+        emit(q, lambda: Q[q].dma_start(ap(o), src), [o], [], (sem, 16, 16))
+
+    sent = [0]
+    engines = len(topo.engines(core, nxt))
+    rid, pid = topo.addr(nxt)[:2]
+
+    def send(o, a, sem):
+        need = {}
+        for h in hist.get(a[0], ()):
+            if meet(h, a) and h[3]:
+                need[h[4]] = max(need.get(h[4], 0), h[5])
+        for src in need:
+            wait("g", src, need[src])
+        g.remote_dma(out_ap=ap(o), in_ap=ap(a), remote_sem=T.sem[sem], local_sem=T.sem["loc"], pid=pid, routing_id=rid,
+                     dma_engine_mask=topo.mask(core, nxt))
+        sent[0] += engines
+
+    def send_codes(o, os, a, s, n, sem):
+        send(R(o, 0, n, 1, None, dt.uint8), R(a, 0, n, 1, None, dt.uint8), sem)
+        send(R(os, 0, n), R(s, 0, n), sem)
+
+    lands("au", 2 * engines, [R("UP", 0, 128), R("UPS", 0, 128)])
+    for r in range(ROUNDS):
+        lands("aq%d" % r, 2 * engines, [R("LQ%d" % r, 0, 256), R("LS%d" % r, 0, 256)])
+        lands("al%d" % r, engines, [R("LP%d" % r, 0, 4)])
+
+    load("y", R("XT", 0, 768), T.x[:], "dx")
+    load("s", R("UT", 0, 512), T.u[:], "du")
+    load("y", R("WQ", 0, 512, 1, None, dt.uint8), T.wc[:], "dw")
+    load("s", R("WS", 0, 512), T.ws[:], "dws")
+    load("y", R("VT", 0, 512), T.v[:], "dv")
+
+    x = R
+    iota(x("PI", 0, 1), [[1, 1]], 0, 1)
+    iota(x("UI", 0, 8), [[16, 8]])
+    iota(R("JM", 0, 256), [[0, 16], [1, 16]])
+    iota(x("M16"), [[16, 16]])
+    iota(R("IOTA", 0, 512), [[1, 512]])
+    iota(R("HRA", 0, 192), [[4, 64], [1, 3]])
+    iota(x("GM", 0, 32), [[1, 2], [0, 16]])
+    iota(x("PAR", 0, 32), [[0, 16], [1, 2]])
+    iota(x("C1C", 0, 32), [[0, 8], [1, 4]])
+    iota(x("C12"), [[12, 16]], -192)
+    iota(x("C16"), [[16, 16]], 16)
+    iota(x("HBP"), [[-4, 16]], -4 - 192)
+    iota(R("SEQ", 192, 208), [[0, 16]], 512)
+    iota(R("SEQO", 192, 208), [[0, 16]], -1)
+    iota(R("XC", 192, 208), [[0, 16]])
+    iota(x("CSMB", 0, 8), [[0, 8]], -192)
+    for n in ("ARB", "D1", "I0", "EB", "C64I"):
+        iota(x(n, 0, 40), [[0, 40]])
+    fill(R("ONEB", 0, 512), 1.0)
+
+    def unit(b):
+        o = R("E%d" % b, 0, 512)
+        emit("g", lambda: g.affine_select(ap(o), ap(R("ONEB", 0, 512)), [[-1, 512]], A.is_equal, 0.0, b, 4), [o], [R("ONEB", 0, 512)])
+
+    for b in range(4):
+        unit(b)
+
+    cp(x("UL", 0, 8), x("UI", 0, 8))
+    ts(x("SI", 0, 1), x("PI", 0, 1), 15, None, A.bitwise_and)
+    ts(R("RST", 0, 256), R("JM", 0, 256), 0.0, None, A.not_equal)
+    cp(x("SP", 0, 1), x("SI", 0, 1))
+    s = x("SP", 0, 1)
+    ts(R("RMIN", 0, 192), R("RST", 0, 192), 2 * BIG, -BIG, A.mult, A.add)
+    ts(R("MASK", 0, 256), R("JM", 0, 256), s, None, A.is_equal)
+    fill(R("SEQS", 192, 208), 192.0)
+    ts(R("DMASK", 0, 192), R("MASK", 0, 192), 2 * BIG, -BIG, A.mult, A.add)
+
+    MASK = lambda n: R("MASK", 0, n)
+    RST = lambda n: R("RST", 0, n)
+
+    def own(o, n=192):
+        return R(o, 15, n, 16)
+
+    act(x("IW"), x("M16"), IDENT, 1.0, s)
+    quant("QU", "QUS", "UT", 128)
+    quant("QX", "QXS", "XT", 192)
+    cp(R("UR", 0, 128, 1, None, dt.uint32), R("QU", 0, 128, 1, R("UL", 0, 8), dt.uint32))
+    cp(R("URS", 0, 128), R("QUS", 0, 128, 1, R("UL", 0, 8)))
+    mm("PP", "UR", "URS", "QX", "QXS", 192)
+    send_codes("UP", "UPS", "UR", "URS", 128, "au")
+    act(R("SC", 0, 192), R("PP", 0, 192))
+    cp(x("KI"), x("IW"))
+    fill(R("XT", 768, 832), 0.0)
+    ts(x("KA4"), x("KI"), 2, None, A.arith_shift_right)
+    ts(x("KB4"), x("KI"), 3, None, A.bitwise_and)
+    ts(x("KI0"), x("KA4"), 3.0, -192.0, A.mult, A.add)
+    ts(x("INV"), x("KB4"), 2.5, None, A.is_lt)
+    tt(x("ENC"), x("KI0"), x("KB4"), A.add)
+    ts(x("H3"), x("IW"), 1.0 / 3, -1.0 / 3, A.mult, A.add)
+    tt(x("EN2"), x("ENC"), x("INV"), A.mult)
+    tt(x("M17"), x("IW"), x("H3"), A.add)
+    ts(x("QVA"), x("EN2"), 192.0, None, A.add)
+    tt(R("TMP", 0, 192), R("SC", 0, 192), R("DMASK", 0, 192), A.min)
+
+    def ranks():
+        scan(R("Z", 0, 192), R("RMIN", 0, 192), R("TMP", 0, 192), A.min, A.max, -BIG)
+        for c in range(12):
+            k = R("Z", 16 * c + 15, 16 * c + 16)
+            e = 16 * c + 16
+            ts(R("CMP", 192 * c, 192 * c + e), R("SC", 0, e), k, None, A.is_le)
+            if e < 192:
+                ts(R("CMP", 192 * c + e, 192 * c + 192), R("SC", e, 192), k, None, A.is_lt)
+            total(x("CNT", c, c + 1), R("CMP", 192 * c, 192 * c + 192), 192)
+        tt(R("EQR", 0, 192), R("Z", 0, 192), R("SC", 0, 192), A.is_equal)
+
+    def ranks_end():
+        tt(x("RK", 0, 12), x("CNT", 0, 12), own("YS"), A.subtract)
+        cp(x("RKU", 0, 12), x("RK", 0, 12))
+
+    ranks()
+    cp(x("HUA", 0, 12), x("M17", 0, 12))
+    scan(R("YS", 0, 192), RST(192), R("EQR", 0, 192))
+    ts(x("PHI", 0, 1), x("PI", 0, 1), 4, 1, A.arith_shift_right, A.bitwise_and)
+    ts(x("I2", 0, 1), x("SI", 0, 1), 12, None, A.bitwise_and)
+    cp(x("PH", 0, 1), x("PHI", 0, 1))
+    cp(x("XL", 0, 1), x("I2", 0, 1))
+    ts(x("XL", 1, 2), x("I2", 0, 1), 4.0, None, A.add)
+    ts(x("AL", 0, 1), x("I2", 0, 1), 3.0, None, A.add)
+    ts(x("GM", 0, 32), x("GM", 0, 32), x("PH", 0, 1), None, A.is_equal)
+    ranks_end()
+    cp(R("SEQS", 0, 192, 1, x("RKU", 0, 12)), R("IOTA", 0, 192))
+    tt(R("TMY", 0, 256), R("SEQS", 0, 208, 1, x("QVA")), MASK(256), A.mult)
+    scan(R("YS", 0, 256), RST(256), R("TMY", 0, 256))
+    for t in range(4):
+        ts(R("OFF", 16 * t, 16 * t + 16), own("YS", 256), 4.0, float(t), A.mult, A.add)
+    for t in range(4):
+        o, a = R("FA", t, W64, 4), R("XT", 0, 784, 1, R("OFF", 16 * t, 16 * t + 16))
+        if t < 2:
+            act(o, a)
+        else:
+            cp(o, a)
+
+    F, Fn = "FA", "FB"
+    HR, HRn = "HRA", "HRB"
+    HU, HUn = "HUA", "HUB"
+    QV, QVn = "QVA", "QVB"
+    KA, KAn = "KA", "KB"
+
+    def keys_start():
+        cp(R("KA", 0, 192, 1, x("RKU", 0, 12)), R("SC", 0, 192))
+        fill(R("ONE", 0, 256), 1.0)
+        fill(R("ZERO", 0, 256), 0.0)
+        fill(R("BIGS", 0, 64), BIG)
+
+    def scalar_constants():
+        for n in range(4):
+            act(R("TP%d" % n, 512, 528), R("ZERO", 0, 16))
+        act(x("RST4"), x("C1C"), SIGN)
+        act(x("C1C", 16, 32), x("C1C", 16, 32), COPY, 0.25)
+        act(x("C1C", 0, 16), x("C1C", 0, 16), IDENT, -0.25, 1.0)
+        act(x("C257"), x("IW"), IDENT, -1.0 / BIG, -257.0 / BIG)
+        act(x("JW1", 0, 4), x("IW", 0, 4), IDENT, 1.0, 1.0)
+        act(x("S16", 0, 1), s, COPY, 1.0 / 16)
+        act(x("S161", 0, 1), s, IDENT, 1.0 / 16, 1.0 / 16)
+        act(x("D0A", 0, 32), x("PAR", 0, 32), COPY, x("S16", 0, 1))
+        act(x("D0B", 0, 32), x("PAR", 0, 32), COPY, x("S161", 0, 1))
+        act(x("C64I", 1, 32, 2), x("IW"), IDENT, 1.0, 64.0)
+        act(x("HBB", 0, 1), s, IDENT, 12.0 * BIG, 11.5 * BIG)
+
+    keys = keys_start
+
+    for r in range(ROUNDS):
+        last = r == ROUNDS - 1
+        qt, qts, lq, ls, lw, lp = ["%s%d" % (n, r) for n in ("QT", "QTS", "LQ", "LS", "LW", "LP")]
+        quant("QF", "QFS", F, 256)
+        for b in range(4):
+            mm("PS%d" % b, "WQ", "WS", "QF", "QFS", 256, 128 * b)
+        for b in range(4):
+            if b < 2:
+                ts(R("G%d" % b, 0, 256), R(F, b, W64, 4), 64.0, None, A.mult)
+            else:
+                act(R("G%d" % b, 0, 256), R(F, b, W64, 4), COPY, 64.0)
+        for b in range(4):
+            tt(R("AD%d" % b, 0, 256), R("PS%d" % b, 0, 256), R("G%d" % b, 0, 256), A.add)
+            if b < 2:
+                act(R("TI", b, W64, 4), R("AD%d" % b, 0, 256), COPY, 0.015625)
+        for b in (2, 3):
+            ts(R("TI", b, W64, 4), R("AD%d" % b, 0, 256), 0.015625, None, A.mult)
+        quant(qt, qts, "TI", 256)
+        mm("PP", "UR", "URS", qt, qts)
+        send_codes(lq, ls, qt, qts, 256, "aq%d" % r)
+        keys()
+        act(R("PR", 0, 256), R("PP", 0, 256))
+        hu = x(HU, 0, 12)
+        tt(R("TMP", 0, 192), R("PR", 0, 256, 1, hu), R("DMASK", 0, 192), A.min)
+        act(R("SC", 0, 192), R("PR", 0, 256, 1, hu))
+        ranks()
+        tt(R("TM2", 0, 192), R(KA, 0, 192), MASK(192), A.mult)
+        scan(R("YS", 0, 192), RST(192), R("EQR", 0, 192))
+        scan(R("KWS", 0, 192), RST(192), R("TM2", 0, 192))
+        act(R("FLB", 0, 256), R("ZERO", 0, 256))
+        if r == 0:
+            scalar_constants()
+            for b in range(4):
+                quant("EQ%d" % b, "EQS%d" % b, "E%d" % b, 128)
+        ranks_end()
+        cp(R("LROW", 0, 192, 1, x("RKU", 0, 12)), R(HR, 0, 192))
+        ts(x("LFN", 0, 12), x("RK", 0, 12), 63.5, -BIG, A.is_lt, A.mult)
+        tt(R("TMP", 0, 64), R("LROW", 0, 64), MASK(64), A.mult)
+        tt(x("KWB", 0, 12), own("KWS"), x("LFN", 0, 12), A.add)
+        scan(R("LL", 0, 64), RST(64), R("TMP", 0, 64))
+        tt(x("LF3", 0, 12), x("LFN", 0, 12), x("C257", 0, 12), A.mult)
+        cp(R(lw, 0, 4), own("LL", 64))
+        send(R(lp, 0, 4), R(lw, 0, 4), "al%d" % r)
+        act(R("LBM", 0, 192), R("IOTA", 0, 192), IDENT, -BIG, x("HBB", 0, 1))
+        mm("PQ", "UP", "UPS", lq, ls)
+        cp(R("FLB", 0, 256, 1, R(lw, 0, 4)), R("BIGS", 0, 64))
+        act(R("SF", 0, 192), R("FLB", 0, 256, 1, hu), IDENT, -1.0 / BIG, 1.0)
+        act(R("SFP", 0, 256), R("FLB", 0, 256), IDENT, -1.0 / BIG, 1.0)
+        act(R("PPR", 0, 256), R("PQ", 0, 256))
+        for b in range(4):
+            mm("PD%d" % (b % 2), "EQ%d" % b, "EQS%d" % b, lq, ls)
+            act(R("TP%d" % b, 256, 512), R("PD%d" % (b % 2), 0, 256))
+        tt(R("KST", 0, 192), R("FLB", 0, 256, 1, hu), R(KA, 0, 192), A.add)
+        scan(R("CCS", 0, 192), R("ONE", 0, 192), R("SF", 0, 192))
+        tt(R("LBK", 0, 192), R("LBM", 0, 192), R("KST", 0, 192), A.max)
+        tt(R("XC", 0, 192), R("CCS", 0, 192), R("SF", 0, 192), A.mult)
+        scan(R("CSP", 0, 256), R("ONE", 0, 256), R("SFP", 0, 256))
+        tt(R("TMY", 0, 256), R("XC", 0, 208, 1, x(QV)), MASK(256), A.mult)
+        tt(x("CSMB", 1, 17), own("CSP", 256), x("HBP"), A.add)
+        tt(R("TM2", 0, 192), R("XC", 0, 192), MASK(192), A.mult)
+        tt(x("NCM"), x("CSMB"), x("CSMB", 1, 17), A.subtract)
+        act(x("TH"), x("NCM"), RELU, 1.0, 14.0)
+        scan(R("XWS", 0, 256), RST(256), R("TMY", 0, 256))
+        act(x("XM"), own("XWS", 256), IDENT, 1.0, -193.0)
+        red(x("LB", 0, 1), R("LBK", 0, 192), A.min)
+        scan(R("XCS", 0, 192), RST(192), R("TM2", 0, 192))
+        ts(x("XV"), own("XWS", 256), 0.0, None, A.is_gt)
+        tt(x("TB", 0, 12), own("XCS"), x("LF3", 0, 12), A.add)
+        if last:
+            act(R("HROL", 0, 192), R(HR, 0, 192))
+            act(R("HROL", 192, 256), R("IOTA", 256, 320))
+            quant("QVC", "QVS", "VT", 128)
+        lpo = R(lp, 0, 4)
+        arr = R(KA, 192, 256)
+        act(arr, R("PPR", 0, 256, 1, lpo))
+        tt(R("TMP", 0, 64), R("PPR", 0, 256, 1, lpo), MASK(64), A.mult)
+        ts(R("ARC", 0, 64), arr, x("LB", 0, 1), None, A.is_lt)
+        scan(R("AOS", 0, 64), RST(64), R("TMP", 0, 64))
+        red(x("AR1", 0, 1), R("ARC", 0, 64), A.add)
+        act(R(HR, 192, 256), R("IOTA", 256, 512, 1, lpo))
+
+        def cmp_stay(c):
+            ts(R("CMN", 192 * c, 192 * c + 192), R("KST", 0, 192), R("AOS", 16 * c + 15, 16 * c + 16), None, A.is_le)
+            total(x("TT", 12 + c, 13 + c), R("CMN", 192 * c, 192 * c + 192), 192)
+
+        def cmp_arr(c):
+            q = R("CMQ", 64 * c, 64 * c + 64)
+            if c >= 12 - ON_SCALAR:
+                act(q, arr, RELU, -1.0, x("KWB", c, c + 1))
+                total(x("AC0", c, c + 1), q, 64, SIGN)
+            else:
+                ts(q, arr, x("KWB", c, c + 1), None, A.is_lt)
+                total(x("AC0", c, c + 1), q, 64)
+
+        compares = [lambda c=c: cmp_stay(c) for c in range(4)] + [lambda c=c: cmp_arr(c) for c in range(12)]
+        sel = R("S4", 0, 16, 1, x("AL", 0, 1))
+        tu = x("TU")
+        windows = [
+            lambda: ts(x("B32", 0, 32), x("GM", 0, 32), x("AR1", 0, 1), None, A.mult),
+            lambda: turn(x("B32T", 0, 32), x("B32", 0, 32)),
+            lambda: tt(x("ARB", 1, 17), x("B32T", 0, 16), x("B32T", 16, 32), A.add),
+            lambda: tt(x("EB", 0, 17), x("ARB", 0, 17), x("CSMB", 0, 17), A.add),
+            lambda: tt(x("AX"), x("ARB", 1, 17), x("ARB", 0, 16), A.subtract),
+            lambda: tt(x("X2", 0, 32), R("EB", 0, 24, 1, x("XL", 0, 2)), x("C1C", 0, 32), A.mult),
+            lambda: tt(x("BA"), x("AX"), x("TH"), A.is_gt),
+            lambda: tt(x("CN4", 0, 4), x("EB", 4, 17, 4), x("EB", 0, 13, 4), A.subtract),
+            lambda: tt(x("E64"), x("X2", 0, 16), x("X2", 16, 32), A.add),
+            lambda: scan(x("S4"), x("RST4"), x("BA"), A.mult, A.max),
+            lambda: ts(x("BAD4", 0, 4), x("CN4", 0, 4), 52.5, None, A.is_gt),
+            lambda: tt(x("EQD"), x("E64"), x("EB", 0, 16), A.subtract),
+            lambda: tt(x("ENI"), x("ARB", 0, 16), x("XM"), A.add),
+            lambda: tt(x("ZX4", 0, 4), x("BAD4", 0, 4), x("S4", 3, 16, 4), A.mult),
+            lambda: tt(x("EP1"), sel, x("EQD"), A.mult),
+            lambda: tt(x("NI"), sel, x("AX"), A.add),
+            lambda: red(x("S256", 0, 1), x("ZX4", 0, 4), A.max),
+            lambda: tt(x("EP1"), x("EP1"), x("EB", 0, 16), A.add),
+            lambda: tt(x("EN2"), x("ENI"), x("XV"), A.mult),
+            lambda: tt(x("CE3"), x("C12"), x("EP1"), A.subtract),
+            lambda: ts(x("I0", 1, 32, 2), x("NI"), x("S256", 0, 1), 0.0, A.add, A.is_equal),
+            lambda: ts(x("EP3"), x("CE3"), x("S256", 0, 1), None, A.mult),
+            lambda: tt(x("D1", 1, 33, 2), x("EP1"), x("EP3"), A.add),
+            lambda: tt(x("D1", 0, 32, 2), x("D1", 3, 35, 2), x("D1", 1, 33, 2), A.subtract),
+            lambda: scan(x("UA", 0, 32), x("D0A", 0, 32), x("D1", 0, 32)),
+            lambda: scan(x("UB", 0, 32), x("D0B", 0, 32), x("D1", 0, 32)),
+            lambda: ts(x("QI"), x("UA", 1, 32, 2), UP_, None, A.add),
+            lambda: tt(x("TT", 12, 16), x("JW1", 0, 4), x("TT", 12, 16), A.add),
+            lambda: tt(x("VL"), x("UB", 1, 32, 2), x("QI"), A.is_gt),
+            lambda: tt(x("TT", 0, 12), x("TB", 0, 12), x("AC0", 0, 12), A.add),
+            lambda: tt(x("I1", 1, 32, 2), x("VL"), x("QI"), A.mult),
+            lambda: ts(tu, x("TT"), -1.0, None, A.add),
+            lambda: tt(x("I1", 0, 32, 2), x("EN2"), x("I1", 1, 32, 2), A.subtract),
+            lambda: cp(R("SEQ", 0, 448, 1, tu), R(HR, 0, 256)),
+            lambda: scan(x("UX", 0, 32), x("I0", 0, 32), x("I1", 0, 32)),
+            lambda: ts(x("HBI"), x("D1", 3, 35, 2), UP_, None, A.add),
+            lambda: ts(x(QVn), x("UX", 1, 32, 2), 192.0, None, A.add),
+            lambda: ts(x("UX", 0, 32, 2), x("UX", 1, 32, 2), 0.0, None, A.is_equal),
+        ]
+        while compares or windows:
+            if windows:
+                windows.pop(0)()
+            if compares:
+                compares.pop(0)()
+        for b in range(4):
+            act(R("TP%d" % b, 0, 256), R("AD%d" % b, 0, 256), COPY, 0.015625)
+        tt(R("TMY", 0, 256), R("SEQ", 0, 208, 1, x(QVn)), MASK(256), A.mult)
+        scan(x("UY", 0, 32), x("C64I", 0, 32), x("UX", 0, 32))
+        scan(R("YS", 0, 256), RST(256), R("TMY", 0, 256))
+        ts(x("QDU"), x("UY", 1, 32, 2), 192.0, None, A.add)
+        cp(x("OFY"), own("YS", 256))
+        for t in range(4):
+            o, a = R(Fn, t, W64, 4), R("TP%d" % t, 0, 528, 1, x("OFY"))
+            if last and t == 3:
+                cp(o, a)
+            else:
+                act(o, a)
+        if not last:
+            cp(R(HRn, 0, 512, 1, x("QDU")), R("IOTA", 0, 256))
+            tt(x("HBP"), x("HBI"), x("C16"), A.subtract)
+            tt(R("TM2", 0, 192), R(HRn, 0, 192), MASK(192), A.mult)
+            tt(x("M17"), x("HBI"), MASK(16), A.mult)
+            scan(R("YS", 0, 192), RST(192), R("TM2", 0, 192))
+            red(x("HB1", 0, 1), x("M17"), A.add)
+            cp(x(HUn, 0, 12), own("YS"))
+            ts(x("HBB", 0, 1), x("HB1", 0, 1), 191.5, BIG, A.add, A.mult)
+
+        def keys(KA=KA, KAn=KAn):
+            cp(R(KAn, 0, 448, 1, x("TU")), R(KA, 0, 256))
+
+        F, Fn, HR, HRn, HU, HUn, QV, QVn, KA, KAn = Fn, F, HRn, HR, HUn, HU, QVn, QV, KAn, KA
+
+    stored = [0]
+
+    def store(q, dst, a, src):
+        stored[0] += 1
+        emit(q, lambda: Q[q].dma_start(dst, src), [], [a], ("dout", 16 * stored[0], 16))
+
+    cp(R("SEQO", 0, 448, 1, x("TU")), R("HROL", 0, 256))
+    quant("QF", "QFS", F, 256)
+    mm("PP", "QVC", "QVS", "QF", "QFS")
+    cp(R("OLR", 0, 256), R("SEQO", 0, 208, 1, x(QV)))
+    act(R("YO", 0, 256), R("PP", 0, 256))
+    qf = R("QF", 0, 256, 1, None, dt.uint8)
+    store("y", T.oc[:, 0:W64], qf, ap(qf))
+    for k in range(4):
+        store("y", T.osc[4 * k:4 * k + 4, 0:256], R("QFS", 0, 256), T.QFS[32 * k:32 * k + 4, 0:256])
+    store("s", T.y[:, 0:256], R("YO", 0, 256), ap(R("YO", 0, 256)))
+    store("y", T.ol[:, 0:256], R("OLR", 0, 256), T.OLR[0:128:16, 0:256])
+
+    for q in ("v", "s", "t", "g"):
+        if known["g"].get(q, 0) < cnt[q]:
+            g.wait_ge(T.sem[sem_of[q]], cnt[q])
+    for n in ("dx", "du", "dw", "dws", "dv"):
+        g.wait_ge(T.sem[n], 16)
+    g.wait_ge(T.sem["dout"], 16 * stored[0])
+    g.wait_ge(T.sem["loc"], sent[0])
+    g.wait_ge(T.sem["au"], 2 * engines)
+    for r in range(ROUNDS):
+        g.wait_ge(T.sem["aq%d" % r], 2 * engines)
+        g.wait_ge(T.sem["al%d" % r], engines)

@@ -9,7 +9,7 @@ BIG = 2.0 ** 96
 ROUNDS = 3
 W64 = 4 * 256
 UP_ = 0.5 - 1.0 / 512
-ON_SCALAR = 8
+ON_SCALAR = 3
 
 SCRATCH = {}
 
@@ -38,11 +38,12 @@ _decl("QF QT0 QT1 QT2 LQ0 LQ1 LQ2", "sbuf", [128, 256], "float8_e4m3fn_x4")
 _decl("QFS QTS0 QTS1 QTS2 LS0 LS1 LS2", "sbuf", [128, 256], "uint8")
 _decl("PS0 PS1 PS2 PS3 PP PQ PD0 PD1", "psum", [128, 512], "float32")
 _decl("IOTA HRA HRB", "sbuf", [128, 512], "float32")
-_decl("JM MASK DMASK RST RMIN ONE ZERO TMP TMY TM2 YS PR PPR FLB SFP CSP XWS OLR HROL YO", "sbuf", [128, 256], "float32")
+_decl("JM MASK DMASK RST RMIN ONE ZERO TMP TMY YS PR PPR FLB SFP CSP XWS OLR HROL YO", "sbuf", [128, 256], "float32")
 _decl("KA KB SEQ SEQO", "sbuf", [128, 448], "float32")
 _decl("SEQS XC", "sbuf", [128, 208], "float32")
-_decl("SC Z EQR LROW SF CCS KST KWS XCS LBM LBK", "sbuf", [128, 192], "float32")
+_decl("SC Z EQR LROW SF CCS KST LBM LBK", "sbuf", [128, 192], "float32")
 _decl("ARR64", "sbuf", [128, 256], "float32")
+_decl("KW XCW HW", "sbuf", [128, 16], "float32")
 SMALL = ("EB D1 ARB CSMB GM B32 B32T X2 PAR C1C D0A D0B UA UB I0 I1 UX C64I UY C12 RST4 C16 IW C257 M16 M17 CNT RK LFN KWB "
          "LF3 TB XM XV NCM TH HBP AX BA S4 E64 EQD EP1 CE3 EP3 VL NI ENI EN2 TT JW1 KI0 ENC INV AC0 SP PH LB AR1 S256 HBB HB1 "
          "S16 S161 CN4 BAD4 ZX4").split()
@@ -56,7 +57,7 @@ PIECE.update({n: ("INTS", 16 * i) for i, n in enumerate("PI SI PHI I2 KI KA4 KB4
 PIECE.update({n: ("LISTS", 16 * i) for i, n in enumerate("RKU HUA HUB QVA QVB QDU TU XL AL UL OFY".split())})
 PIECE.update({n: ("ARR64", 64 * i) for i, n in enumerate("LL AOS ARC BIGS".split())})
 
-SEMAPHORES = ["sv", "ss", "st", "sg", "dx", "du", "dw", "dws", "dv", "dout", "loc", "au",
+SEMAPHORES = ["sv", "ss", "st", "sg", "dx", "du", "dw", "dws", "dv", "dout", "loc", "au", "fk", "fx", "fh",
               "aq0", "aq1", "aq2", "al0", "al1", "al2"]
 
 
@@ -208,6 +209,14 @@ def rank_program(g, core, T, topo):
     def load(q, o, src, sem):
         emit(q, lambda: Q[q].dma_start(ap(o), src), [o], [], (sem, 16, 16))
 
+    folded = {n: 0 for n in ("fk", "fx", "fh")}
+
+    def dma_fold(o, a, n, sem):
+        folded[sem] += n
+        for c in range(n // 16):
+            src = T[a][0:128:16, 16 * c:16 * c + 16]
+            emit("y", lambda: g.sync.dma_start(ap(R(o, c, c + 1)), src), [R(o, c, c + 1)], [R(a, 16 * c, 16 * c + 16)], (sem, folded[sem], 16))
+
     sent = [0]
     engines = len(topo.engines(core, nxt))
     rid, pid = topo.addr(nxt)[:2]
@@ -239,9 +248,9 @@ def rank_program(g, core, T, topo):
     load("y", R("VT", 0, 512), T.v[:], "dv")
 
     x = R
+    iota(R("JM", 0, 256), [[0, 16], [1, 16]])
     iota(x("PI", 0, 1), [[1, 1]], 0, 1)
     iota(x("UI", 0, 8), [[16, 8]])
-    iota(R("JM", 0, 256), [[0, 16], [1, 16]])
     iota(x("M16"), [[16, 16]])
     iota(R("IOTA", 0, 512), [[1, 512]])
     iota(R("HRA", 0, 192), [[4, 64], [1, 3]])
@@ -257,6 +266,8 @@ def rank_program(g, core, T, topo):
     iota(x("CSMB", 0, 8), [[0, 8]], -192)
     for n in ("ARB", "D1", "I0", "EB", "C64I"):
         iota(x(n, 0, 40), [[0, 40]])
+    iota(R("ONE", 0, 256), [[0, 256]], 1)
+    iota(R("ZERO", 0, 256), [[0, 256]])
     fill(R("ONEB", 0, 512), 1.0)
 
     def unit(b):
@@ -266,15 +277,16 @@ def rank_program(g, core, T, topo):
     for b in range(4):
         unit(b)
 
-    cp(x("UL", 0, 8), x("UI", 0, 8))
-    ts(x("SI", 0, 1), x("PI", 0, 1), 15, None, A.bitwise_and)
     ts(R("RST", 0, 256), R("JM", 0, 256), 0.0, None, A.not_equal)
+    ts(x("SI", 0, 1), x("PI", 0, 1), 15, None, A.bitwise_and)
+    cp(x("UL", 0, 8), x("UI", 0, 8))
     cp(x("SP", 0, 1), x("SI", 0, 1))
     s = x("SP", 0, 1)
     ts(R("RMIN", 0, 192), R("RST", 0, 192), 2 * BIG, -BIG, A.mult, A.add)
     ts(R("MASK", 0, 256), R("JM", 0, 256), s, None, A.is_equal)
     fill(R("SEQS", 192, 208), 192.0)
     ts(R("DMASK", 0, 192), R("MASK", 0, 192), 2 * BIG, -BIG, A.mult, A.add)
+    fill(R("BIGS", 0, 64), BIG)
 
     MASK = lambda n: R("MASK", 0, n)
     RST = lambda n: R("RST", 0, n)
@@ -303,7 +315,7 @@ def rank_program(g, core, T, topo):
     ts(x("QVA"), x("EN2"), 192.0, None, A.add)
     tt(R("TMP", 0, 192), R("SC", 0, 192), R("DMASK", 0, 192), A.min)
 
-    def ranks():
+    def ranks(others=()):
         scan(R("Z", 0, 192), R("RMIN", 0, 192), R("TMP", 0, 192), A.min, A.max, -BIG)
         for c in range(12):
             k = R("Z", 16 * c + 15, 16 * c + 16)
@@ -312,6 +324,8 @@ def rank_program(g, core, T, topo):
             if e < 192:
                 ts(R("CMP", 192 * c + e, 192 * c + 192), R("SC", e, 192), k, None, A.is_lt)
             total(x("CNT", c, c + 1), R("CMP", 192 * c, 192 * c + 192), 192)
+            if c < len(others):
+                others[c]()
         tt(R("EQR", 0, 192), R("Z", 0, 192), R("SC", 0, 192), A.is_equal)
 
     def ranks_end():
@@ -347,12 +361,6 @@ def rank_program(g, core, T, topo):
     QV, QVn = "QVA", "QVB"
     KA, KAn = "KA", "KB"
 
-    def keys_start():
-        cp(R("KA", 0, 192, 1, x("RKU", 0, 12)), R("SC", 0, 192))
-        fill(R("ONE", 0, 256), 1.0)
-        fill(R("ZERO", 0, 256), 0.0)
-        fill(R("BIGS", 0, 64), BIG)
-
     def scalar_constants():
         for n in range(4):
             act(R("TP%d" % n, 512, 528), R("ZERO", 0, 16))
@@ -368,7 +376,7 @@ def rank_program(g, core, T, topo):
         act(x("C64I", 1, 32, 2), x("IW"), IDENT, 1.0, 64.0)
         act(x("HBB", 0, 1), s, IDENT, 12.0 * BIG, 11.5 * BIG)
 
-    keys = keys_start
+    keys = [lambda: cp(R("KA", 0, 192, 1, x("RKU", 0, 12)), R("SC", 0, 192))]
 
     for r in range(ROUNDS):
         last = r == ROUNDS - 1
@@ -387,69 +395,76 @@ def rank_program(g, core, T, topo):
                 act(R("TI", b, W64, 4), R("AD%d" % b, 0, 256), COPY, 0.015625)
         for b in (2, 3):
             ts(R("TI", b, W64, 4), R("AD%d" % b, 0, 256), 0.015625, None, A.mult)
+
+        def plane(b):
+            act(R("TP%d" % b, 0, 256), R("AD%d" % b, 0, 256), COPY, 0.015625)
+
+        def unpack(b):
+            mm("PD%d" % (b % 2), "EQ%d" % b, "EQS%d" % b, lq, ls)
+            act(R("TP%d" % b, 256, 512), R("PD%d" % (b % 2), 0, 256))
+
         quant(qt, qts, "TI", 256)
         mm("PP", "UR", "URS", qt, qts)
         send_codes(lq, ls, qt, qts, 256, "aq%d" % r)
-        keys()
+        keys[0]()
+        dma_fold("KW", KA, 192, "fk")
+        if r > 0:
+            cp(x(HU, 0, 12), x("HW", 0, 12))
+        plane(0)
+        plane(1)
         act(R("PR", 0, 256), R("PP", 0, 256))
         hu = x(HU, 0, 12)
         tt(R("TMP", 0, 192), R("PR", 0, 256, 1, hu), R("DMASK", 0, 192), A.min)
         act(R("SC", 0, 192), R("PR", 0, 256, 1, hu))
-        ranks()
-        tt(R("TM2", 0, 192), R(KA, 0, 192), MASK(192), A.mult)
+        plane(2)
+        plane(3)
+        ranks(keys[1:])
         scan(R("YS", 0, 192), RST(192), R("EQR", 0, 192))
-        scan(R("KWS", 0, 192), RST(192), R("TM2", 0, 192))
         act(R("FLB", 0, 256), R("ZERO", 0, 256))
         if r == 0:
             scalar_constants()
             for b in range(4):
                 quant("EQ%d" % b, "EQS%d" % b, "E%d" % b, 128)
+        act(R("LBM", 0, 192), R("IOTA", 0, 192), IDENT, -BIG, x("HBB", 0, 1))
+        mm("PQ", "UP", "UPS", lq, ls)
+        act(R("PPR", 0, 256), R("PQ", 0, 256))
+        unpack(0)
+        unpack(1)
         ranks_end()
         cp(R("LROW", 0, 192, 1, x("RKU", 0, 12)), R(HR, 0, 192))
         ts(x("LFN", 0, 12), x("RK", 0, 12), 63.5, -BIG, A.is_lt, A.mult)
         tt(R("TMP", 0, 64), R("LROW", 0, 64), MASK(64), A.mult)
-        tt(x("KWB", 0, 12), own("KWS"), x("LFN", 0, 12), A.add)
-        scan(R("LL", 0, 64), RST(64), R("TMP", 0, 64))
         tt(x("LF3", 0, 12), x("LFN", 0, 12), x("C257", 0, 12), A.mult)
+        scan(R("LL", 0, 64), RST(64), R("TMP", 0, 64))
         cp(R(lw, 0, 4), own("LL", 64))
         send(R(lp, 0, 4), R(lw, 0, 4), "al%d" % r)
-        act(R("LBM", 0, 192), R("IOTA", 0, 192), IDENT, -BIG, x("HBB", 0, 1))
-        mm("PQ", "UP", "UPS", lq, ls)
         cp(R("FLB", 0, 256, 1, R(lw, 0, 4)), R("BIGS", 0, 64))
         act(R("SF", 0, 192), R("FLB", 0, 256, 1, hu), IDENT, -1.0 / BIG, 1.0)
         act(R("SFP", 0, 256), R("FLB", 0, 256), IDENT, -1.0 / BIG, 1.0)
-        act(R("PPR", 0, 256), R("PQ", 0, 256))
-        for b in range(4):
-            mm("PD%d" % (b % 2), "EQ%d" % b, "EQS%d" % b, lq, ls)
-            act(R("TP%d" % b, 256, 512), R("PD%d" % (b % 2), 0, 256))
         tt(R("KST", 0, 192), R("FLB", 0, 256, 1, hu), R(KA, 0, 192), A.add)
-        scan(R("CCS", 0, 192), R("ONE", 0, 192), R("SF", 0, 192))
+        unpack(2)
+        unpack(3)
         tt(R("LBK", 0, 192), R("LBM", 0, 192), R("KST", 0, 192), A.max)
+        scan(R("CCS", 0, 192), R("ONE", 0, 192), R("SF", 0, 192))
+        red(x("LB", 0, 1), R("LBK", 0, 192), A.min)
         tt(R("XC", 0, 192), R("CCS", 0, 192), R("SF", 0, 192), A.mult)
+        dma_fold("XCW", "XC", 192, "fx")
         scan(R("CSP", 0, 256), R("ONE", 0, 256), R("SFP", 0, 256))
         tt(R("TMY", 0, 256), R("XC", 0, 208, 1, x(QV)), MASK(256), A.mult)
         tt(x("CSMB", 1, 17), own("CSP", 256), x("HBP"), A.add)
-        tt(R("TM2", 0, 192), R("XC", 0, 192), MASK(192), A.mult)
-        tt(x("NCM"), x("CSMB"), x("CSMB", 1, 17), A.subtract)
-        act(x("TH"), x("NCM"), RELU, 1.0, 14.0)
         scan(R("XWS", 0, 256), RST(256), R("TMY", 0, 256))
-        act(x("XM"), own("XWS", 256), IDENT, 1.0, -193.0)
-        red(x("LB", 0, 1), R("LBK", 0, 192), A.min)
-        scan(R("XCS", 0, 192), RST(192), R("TM2", 0, 192))
-        ts(x("XV"), own("XWS", 256), 0.0, None, A.is_gt)
-        tt(x("TB", 0, 12), own("XCS"), x("LF3", 0, 12), A.add)
+        tt(x("NCM"), x("CSMB"), x("CSMB", 1, 17), A.subtract)
+        tt(x("KWB", 0, 12), x("KW", 0, 12), x("LFN", 0, 12), A.add)
         if last:
-            act(R("HROL", 0, 192), R(HR, 0, 192))
-            act(R("HROL", 192, 256), R("IOTA", 256, 320))
             quant("QVC", "QVS", "VT", 128)
         lpo = R(lp, 0, 4)
         arr = R(KA, 192, 256)
         act(arr, R("PPR", 0, 256, 1, lpo))
+        act(x("TH"), x("NCM"), RELU, 1.0, 14.0)
         tt(R("TMP", 0, 64), R("PPR", 0, 256, 1, lpo), MASK(64), A.mult)
         ts(R("ARC", 0, 64), arr, x("LB", 0, 1), None, A.is_lt)
         scan(R("AOS", 0, 64), RST(64), R("TMP", 0, 64))
         red(x("AR1", 0, 1), R("ARC", 0, 64), A.add)
-        act(R(HR, 192, 256), R("IOTA", 256, 512, 1, lpo))
 
         def cmp_stay(c):
             ts(R("CMN", 192 * c, 192 * c + 192), R("KST", 0, 192), R("AOS", 16 * c + 15, 16 * c + 16), None, A.is_le)
@@ -480,64 +495,66 @@ def rank_program(g, core, T, topo):
             lambda: scan(x("S4"), x("RST4"), x("BA"), A.mult, A.max),
             lambda: ts(x("BAD4", 0, 4), x("CN4", 0, 4), 52.5, None, A.is_gt),
             lambda: tt(x("EQD"), x("E64"), x("EB", 0, 16), A.subtract),
-            lambda: tt(x("ENI"), x("ARB", 0, 16), x("XM"), A.add),
             lambda: tt(x("ZX4", 0, 4), x("BAD4", 0, 4), x("S4", 3, 16, 4), A.mult),
+            lambda: act(x("XM"), own("XWS", 256), IDENT, 1.0, -193.0),
+            lambda: act(x("XV"), own("XWS", 256), SIGN),
             lambda: tt(x("EP1"), sel, x("EQD"), A.mult),
             lambda: tt(x("NI"), sel, x("AX"), A.add),
             lambda: red(x("S256", 0, 1), x("ZX4", 0, 4), A.max),
             lambda: tt(x("EP1"), x("EP1"), x("EB", 0, 16), A.add),
-            lambda: tt(x("EN2"), x("ENI"), x("XV"), A.mult),
-            lambda: tt(x("CE3"), x("C12"), x("EP1"), A.subtract),
             lambda: ts(x("I0", 1, 32, 2), x("NI"), x("S256", 0, 1), 0.0, A.add, A.is_equal),
+            lambda: tt(x("CE3"), x("C12"), x("EP1"), A.subtract),
+            lambda: tt(x("ENI"), x("ARB", 0, 16), x("XM"), A.add),
             lambda: ts(x("EP3"), x("CE3"), x("S256", 0, 1), None, A.mult),
+            lambda: tt(x("EN2"), x("ENI"), x("XV"), A.mult),
             lambda: tt(x("D1", 1, 33, 2), x("EP1"), x("EP3"), A.add),
+            lambda: tt(x("TB", 0, 12), x("XCW", 0, 12), x("LF3", 0, 12), A.add),
             lambda: tt(x("D1", 0, 32, 2), x("D1", 3, 35, 2), x("D1", 1, 33, 2), A.subtract),
+            lambda: tt(x("TT", 12, 16), x("JW1", 0, 4), x("TT", 12, 16), A.add),
             lambda: scan(x("UA", 0, 32), x("D0A", 0, 32), x("D1", 0, 32)),
             lambda: scan(x("UB", 0, 32), x("D0B", 0, 32), x("D1", 0, 32)),
             lambda: ts(x("QI"), x("UA", 1, 32, 2), UP_, None, A.add),
-            lambda: tt(x("TT", 12, 16), x("JW1", 0, 4), x("TT", 12, 16), A.add),
-            lambda: tt(x("VL"), x("UB", 1, 32, 2), x("QI"), A.is_gt),
             lambda: tt(x("TT", 0, 12), x("TB", 0, 12), x("AC0", 0, 12), A.add),
-            lambda: tt(x("I1", 1, 32, 2), x("VL"), x("QI"), A.mult),
+            lambda: tt(x("VL"), x("UB", 1, 32, 2), x("QI"), A.is_gt),
             lambda: ts(tu, x("TT"), -1.0, None, A.add),
-            lambda: tt(x("I1", 0, 32, 2), x("EN2"), x("I1", 1, 32, 2), A.subtract),
+            lambda: tt(x("I1", 1, 32, 2), x("VL"), x("QI"), A.mult),
             lambda: cp(R("SEQ", 0, 448, 1, tu), R(HR, 0, 256)),
+            lambda: tt(x("I1", 0, 32, 2), x("EN2"), x("I1", 1, 32, 2), A.subtract),
             lambda: scan(x("UX", 0, 32), x("I0", 0, 32), x("I1", 0, 32)),
-            lambda: ts(x("HBI"), x("D1", 3, 35, 2), UP_, None, A.add),
             lambda: ts(x(QVn), x("UX", 1, 32, 2), 192.0, None, A.add),
-            lambda: ts(x("UX", 0, 32, 2), x("UX", 1, 32, 2), 0.0, None, A.is_equal),
         ]
+        act(R(HR, 192, 256), R("IOTA", 256, 512, 1, lpo))
         while compares or windows:
             if windows:
                 windows.pop(0)()
             if compares:
                 compares.pop(0)()
-        for b in range(4):
-            act(R("TP%d" % b, 0, 256), R("AD%d" % b, 0, 256), COPY, 0.015625)
+        if last:
+            act(R("HROL", 0, 192), R(HR, 0, 192))
+            act(R("HROL", 192, 256), R("IOTA", 256, 320))
+        else:
+            ts(x("UX", 0, 32, 2), x("UX", 1, 32, 2), 0.0, None, A.is_equal)
         tt(R("TMY", 0, 256), R("SEQ", 0, 208, 1, x(QVn)), MASK(256), A.mult)
-        scan(x("UY", 0, 32), x("C64I", 0, 32), x("UX", 0, 32))
+        if not last:
+            scan(x("UY", 0, 32), x("C64I", 0, 32), x("UX", 0, 32))
         scan(R("YS", 0, 256), RST(256), R("TMY", 0, 256))
-        ts(x("QDU"), x("UY", 1, 32, 2), 192.0, None, A.add)
+        if not last:
+            ts(x("QDU"), x("UY", 1, 32, 2), 192.0, None, A.add)
         cp(x("OFY"), own("YS", 256))
-        for t in range(4):
-            o, a = R(Fn, t, W64, 4), R("TP%d" % t, 0, 528, 1, x("OFY"))
-            if last and t == 3:
-                cp(o, a)
-            else:
-                act(o, a)
+        for t in range(3):
+            act(R(Fn, t, W64, 4), R("TP%d" % t, 0, 528, 1, x("OFY")))
         if not last:
             cp(R(HRn, 0, 512, 1, x("QDU")), R("IOTA", 0, 256))
-            tt(x("HBP"), x("HBI"), x("C16"), A.subtract)
-            tt(R("TM2", 0, 192), R(HRn, 0, 192), MASK(192), A.mult)
-            tt(x("M17"), x("HBI"), MASK(16), A.mult)
-            scan(R("YS", 0, 192), RST(192), R("TM2", 0, 192))
-            red(x("HB1", 0, 1), x("M17"), A.add)
-            cp(x(HUn, 0, 12), own("YS"))
-            ts(x("HBB", 0, 1), x("HB1", 0, 1), 191.5, BIG, A.add, A.mult)
-
-        def keys(KA=KA, KAn=KAn):
-            cp(R(KAn, 0, 448, 1, x("TU")), R(KA, 0, 256))
-
+            dma_fold("HW", HRn, 192, "fh")
+        cp(R(Fn, 3, W64, 4), R("TP3", 0, 528, 1, x("OFY")))
+        keys = [
+            lambda KA=KA, KAn=KAn: cp(R(KAn, 0, 448, 1, x("TU")), R(KA, 0, 256)),
+            lambda: ts(x("HBI"), x("D1", 3, 35, 2), UP_, None, A.add),
+            lambda: tt(x("HBP"), x("HBI"), x("C16"), A.subtract),
+            lambda: tt(x("M17"), x("HBI"), MASK(16), A.mult),
+            lambda: red(x("HB1", 0, 1), x("M17"), A.add),
+            lambda: ts(x("HBB", 0, 1), x("HB1", 0, 1), 191.5, BIG, A.add, A.mult),
+        ]
         F, Fn, HR, HRn, HU, HUn, QV, QVn, KA, KAn = Fn, F, HRn, HR, HUn, HU, QVn, QV, KAn, KA
 
     stored = [0]
@@ -563,6 +580,8 @@ def rank_program(g, core, T, topo):
             g.wait_ge(T.sem[sem_of[q]], cnt[q])
     for n in ("dx", "du", "dw", "dws", "dv"):
         g.wait_ge(T.sem[n], 16)
+    for n in ("fk", "fx", "fh"):
+        g.wait_ge(T.sem[n], folded[n])
     g.wait_ge(T.sem["dout"], 16 * stored[0])
     g.wait_ge(T.sem["loc"], sent[0])
     g.wait_ge(T.sem["au"], 2 * engines)

from concourse.mybir import dt, AluOpType, AxisListType, ActivationFunctionType

A = AluOpType
COPY = ActivationFunctionType.Copy
IDENT = ActivationFunctionType.Identity
RELU = ActivationFunctionType.Relu
SIGN = ActivationFunctionType.Sign
BIG = 2.0 ** 96
ROUNDS = 3
W64 = 4 * 256
UP_ = 0.5 - 1.0 / 512
ON_SCALAR = 3

SCRATCH = {}


def _decl(names, where, shape, dtype):
    for n in names.split():
        SCRATCH[n] = (where, shape, dtype)


_decl("XT", "sbuf", [128, 832], "bfloat16")
_decl("UT VT E0 E1 E2 E3 ONEB", "sbuf", [128, 512], "bfloat16")
_decl("TI FA FB", "sbuf", [128, 1024], "bfloat16")
_decl("TP0 TP1 TP2 TP3", "sbuf", [128, 528], "bfloat16")
_decl("AD0 AD1 AD2 AD3 G0 G1 G2 G3", "sbuf", [128, 256], "bfloat16")
_decl("CMP", "sbuf", [128, 2304], "bfloat16")
_decl("JNK", "sbuf", [128, 1536], "bfloat16")
_decl("CMQ", "sbuf", [128, 768], "float32")
_decl("CMN", "sbuf", [128, 768], "bfloat16")
_decl("QX", "sbuf", [128, 192], "float8_e4m3fn_x4")
_decl("QXS", "sbuf", [128, 192], "uint8")
_decl("QU QVC UR UP EQ0 EQ1 EQ2 EQ3", "sbuf", [128, 128], "float8_e4m3fn_x4")
_decl("QUS QVS URS UPS EQS0 EQS1 EQS2 EQS3", "sbuf", [128, 128], "uint8")
_decl("WQ", "sbuf", [128, 512], "float8_e4m3fn_x4")
_decl("WS", "sbuf", [128, 512], "uint8")
_decl("QF QT0 QT1 QT2 LQ0 LQ1 LQ2", "sbuf", [128, 256], "float8_e4m3fn_x4")
_decl("QFS QTS0 QTS1 QTS2 LS0 LS1 LS2", "sbuf", [128, 256], "uint8")
_decl("PS0 PS1 PS2 PS3 PP PQ PD0 PD1", "psum", [128, 512], "float32")
_decl("IOTA HRA HRB", "sbuf", [128, 512], "float32")
_decl("JM MASK DMASK RST RMIN ONE ZERO TMP TMY YS PR PPR FLB SFP CSP XWS OLR HROL YO", "sbuf", [128, 256], "float32")
_decl("KA KB SEQ SEQO", "sbuf", [128, 448], "float32")
_decl("SEQS XC", "sbuf", [128, 208], "float32")
_decl("SC Z EQR LROW SF CCS KST LBM LBK", "sbuf", [128, 192], "float32")
_decl("ARR64", "sbuf", [128, 256], "float32")
_decl("KW XCW HW", "sbuf", [128, 16], "float32")
SMALL = ("EB D1 ARB CSMB GM B32 B32T X2 PAR C1C D0A D0B UA UB I0 I1 UX C64I UY C12 RST4 C16 IW C257 M16 M17 CNT RK LFN KWB "
         "LF3 TB XM XV NCM TH HBP AX BA S4 E64 EQD EP1 CE3 EP3 VL NI ENI EN2 TT JW1 KI0 ENC INV AC0 SP PH LB AR1 S256 HBB HB1 "
         "S16 S161 CN4 BAD4 ZX4").split()
_decl("SMALLS", "sbuf", [128, 40 * len(SMALL)], "float32")
_decl("INTS", "sbuf", [128, 16 * 11], "int32")
_decl("LW0 LW1 LW2 LP0 LP1 LP2", "sbuf", [128, 4], "uint16")
_decl("LISTS", "sbuf", [128, 16 * 12], "uint16")
_decl("OFF", "sbuf", [128, 64], "uint16")
PIECE = {n: ("SMALLS", 40 * i) for i, n in enumerate(SMALL)}
PIECE.update({n: ("INTS", 16 * i) for i, n in enumerate("PI SI PHI I2 KI KA4 KB4 UI QI HBI H3".split())})
PIECE.update({n: ("LISTS", 16 * i) for i, n in enumerate("RKU HUA HUB QVA QVB QDU TU XL AL UL OFY".split())})
PIECE.update({n: ("ARR64", 64 * i) for i, n in enumerate("LL AOS ARC BIGS".split())})

SEMAPHORES = ["sv", "ss", "st", "sg", "dx", "du", "dw", "dws", "dv", "dout", "loc", "au", "fk", "fx", "fh",
              "aq0", "aq1", "aq2", "al0", "al1", "al2"]


def R(name, a=0, b=16, st=1, off=None, bc=None):
    n, k = PIECE.get(name, (name, 0))
    return (n, k + a, k + b, st, off, bc)


def rank_program(g, core, T, topo):
    rank = T.rank_of(core)
    if rank is None:
        return
    nxt = T.cores[(rank + 1) % len(T.cores)]

    Q = {"v": g.vector, "s": g.scalar, "t": g.tensor, "g": g, "y": g.sync}
    sem_of = {"v": "sv", "s": "ss", "t": "st", "g": "sg"}
    cnt = {q: 0 for q in Q}
    known = {q: {} for q in Q}
    clocks = {}
    hist = {}

    def ap(r):
        n, a, b, st, off, bc = r
        x = T[n][:, a:b] if st == 1 else T[n][:, a:b:st]
        if bc is not None:
            x = x.bitcast(bc)
        if off is not None:
            x = x.indirect(ap(off))
        return x

    def meet(h, r):
        if h[0] >= r[2] or r[1] >= h[1]:
            return False
        return not (h[2] > 1 and h[2] == r[3] and (h[0] - r[1]) % h[2])

    def wait(q, src, val):
        if known[q].get(src, 0) >= val:
            return
        Q[q].wait_ge(T.sem[sem_of.get(src, src)], val)
        for s, v in clocks[(src, val)].items():
            if known[q].get(s, 0) < v:
                known[q][s] = v

    def psum(n):
        return n in SCRATCH and SCRATCH[n][0] == "psum"

    def note(src, val, writes, reads):
        for w in writes:
            h = hist.setdefault(w[0], [])
            if w[3] == 1 and w[4] is None:
                h[:] = [e for e in h if not (w[1] <= e[0] and e[1] <= w[2])]
            h.append((w[1], w[2], w[3], True, src, val))
        for r in reads:
            hist.setdefault(r[0], []).append((r[1], r[2], r[3], psum(r[0]), src, val))

    def emit(q, call, writes, reads, event=None):
        reads = list(reads)
        for r in list(reads) + list(writes):
            if r[4] is not None:
                reads.append(r[4])
        need = {}
        for r in reads:
            for h in hist.get(r[0], ()):
                if meet(h, r) and h[3] and not (psum(r[0]) and h[4] == q):
                    need[h[4]] = max(need.get(h[4], 0), h[5])
        for w in writes:
            for h in hist.get(w[0], ()):
                if meet(h, w):
                    need[h[4]] = max(need.get(h[4], 0), h[5])
        for src in sorted(need, key=lambda s: -len(clocks[(s, need[s])])):
            wait(q, src, need[src])
        i = call()
        if event is None:
            cnt[q] += 1
            i.then_inc(T.sem[sem_of[q]], 1)
            src, val = q, cnt[q]
        else:
            src, val, inc = event
            i.then_inc(T.sem[src], inc)
        clocks[(src, val)] = dict(known[q])
        clocks[(src, val)][src] = val
        note(src, val, writes, reads)

    def lands(src, val, writes):
        clocks[(src, val)] = {src: val}
        note(src, val, writes, [])

    def isr(x):
        return isinstance(x, tuple)

    def val(x):
        return ap(x) if isr(x) else x

    def tt(o, a, b, op):
        emit("v", lambda: g.vector.tensor_tensor(ap(o), ap(a), ap(b), op), [o], [a, b])

    def ts(o, a, s1, s2, op0, op1=None):
        rd = [a] + [x for x in (s1, s2) if isr(x)]
        if op1 is None:
            emit("v", lambda: g.vector.tensor_scalar(ap(o), ap(a), val(s1), None, op0), [o], rd)
        else:
            emit("v", lambda: g.vector.tensor_scalar(ap(o), ap(a), val(s1), val(s2), op0, op1), [o], rd)

    def cp(o, a):
        emit("v", lambda: g.vector.tensor_copy(ap(o), ap(a)), [o], [a])

    def scan(o, d0, d1, op0=A.mult, op1=A.add, init=0.0):
        emit("v", lambda: g.vector.tensor_tensor_scan(ap(o), ap(d0), ap(d1), init, op0, op1), [o], [d0, d1])

    def red(o, a, op):
        emit("v", lambda: g.vector.tensor_reduce(ap(o), ap(a), AxisListType.X, op), [o], [a])

    def fill(o, c):
        emit("v", lambda: g.vector.memset(ap(o), c), [o], [])

    def turn(o, a):
        emit("v", lambda: g.vector.transpose(ap(o), ap(a)), [o], [a])

    def quant(o, s, a, n):
        o, s, a = R(o, 0, n), R(s, 0, n), R(a, 0, 4 * n)
        emit("v", lambda: g.vector.quantize_mx(ap(o), ap(s), ap(a)), [o, s], [a])

    def act(o, a, func=COPY, scale=1.0, bias=0.0):
        rd = [a] + [x for x in (scale, bias) if isr(x)]
        if func == COPY and not isr(scale) and scale == 1.0:
            emit("s", lambda: g.scalar.activation(ap(o), ap(a), COPY), [o], rd)
        elif func == COPY:
            emit("s", lambda: g.scalar.activation(ap(o), ap(a), COPY, scale=val(scale)), [o], rd)
        else:
            emit("s", lambda: g.scalar.activation(ap(o), ap(a), func, bias=val(bias), scale=val(scale)), [o], rd)

    turns = [0]

    def total(o, a, n, func=COPY):
        j = R("JNK", 192 * (turns[0] % 8), 192 * (turns[0] % 8) + n)
        turns[0] += 1
        emit("s", lambda: g.scalar.activation(ap(j), ap(a), func, accum_out=ap(o)), [j, o], [a])

    def mm(o, l, ls, r, rs, n=256, c=0):
        o, l, ls, r, rs = R(o, 0, n), R(l, c, c + 128), R(ls, c, c + 128), R(r, 0, n), R(rs, 0, n)
        emit("t", lambda: g.tensor.matmul_mx(ap(o), ap(l), ap(ls), ap(r), ap(rs), True, True), [o], [l, ls, r, rs])

    def iota(o, pattern, base=0, cm=0):
        if SCRATCH[o[0]][2] == "int32":
            emit("g", lambda: g.iota(ap(o), pattern, base, cm), [o], [])
        else:
            emit("g", lambda: g.iota(ap(o), pattern, base, cm, allow_small_or_imprecise_dtypes=True), [o], [])

    def load(q, o, src, sem):
        emit(q, lambda: Q[q].dma_start(ap(o), src), [o], [], (sem, 16, 16))

    folded = {n: 0 for n in ("fk", "fx", "fh")}

    def dma_fold(o, a, n, sem):
        folded[sem] += n
        for c in range(n // 16):
            src = T[a][0:128:16, 16 * c:16 * c + 16]
            emit("y", lambda: g.sync.dma_start(ap(R(o, c, c + 1)), src), [R(o, c, c + 1)], [R(a, 16 * c, 16 * c + 16)], (sem, folded[sem], 16))

    sent = [0]
    engines = len(topo.engines(core, nxt))
    rid, pid = topo.addr(nxt)[:2]

    def send(o, a, sem):
        need = {}
        for h in hist.get(a[0], ()):
            if meet(h, a) and h[3]:
                need[h[4]] = max(need.get(h[4], 0), h[5])
        for src in need:
            wait("g", src, need[src])
        g.remote_dma(out_ap=ap(o), in_ap=ap(a), remote_sem=T.sem[sem], local_sem=T.sem["loc"], pid=pid, routing_id=rid,
                     dma_engine_mask=topo.mask(core, nxt))
        sent[0] += engines

    def send_codes(o, os, a, s, n, sem):
        send(R(o, 0, n, 1, None, dt.uint8), R(a, 0, n, 1, None, dt.uint8), sem)
        send(R(os, 0, n), R(s, 0, n), sem)

    lands("au", 2 * engines, [R("UP", 0, 128), R("UPS", 0, 128)])
    for r in range(ROUNDS):
        lands("aq%d" % r, 2 * engines, [R("LQ%d" % r, 0, 256), R("LS%d" % r, 0, 256)])
        lands("al%d" % r, engines, [R("LP%d" % r, 0, 4)])

    load("y", R("XT", 0, 768), T.x[:], "dx")
    load("s", R("UT", 0, 512), T.u[:], "du")
    load("y", R("WQ", 0, 512, 1, None, dt.uint8), T.wc[:], "dw")
    load("s", R("WS", 0, 512), T.ws[:], "dws")
    load("y", R("VT", 0, 512), T.v[:], "dv")

    x = R
    iota(R("JM", 0, 256), [[0, 16], [1, 16]])
    iota(x("PI", 0, 1), [[1, 1]], 0, 1)
    iota(x("UI", 0, 8), [[16, 8]])
    iota(x("M16"), [[16, 16]])
    iota(R("IOTA", 0, 512), [[1, 512]])
    iota(R("HRA", 0, 192), [[4, 64], [1, 3]])
    iota(x("GM", 0, 32), [[1, 2], [0, 16]])
    iota(x("PAR", 0, 32), [[0, 16], [1, 2]])
    iota(x("C1C", 0, 32), [[0, 8], [1, 4]])
    iota(x("C12"), [[12, 16]], -192)
    iota(x("C16"), [[16, 16]], 16)
    iota(x("HBP"), [[-4, 16]], -4 - 192)
    iota(R("SEQ", 192, 208), [[0, 16]], 512)
    iota(R("SEQO", 192, 208), [[0, 16]], -1)
    iota(R("XC", 192, 208), [[0, 16]])
    iota(x("CSMB", 0, 8), [[0, 8]], -192)
    for n in ("ARB", "D1", "I0", "EB", "C64I"):
        iota(x(n, 0, 40), [[0, 40]])
    iota(R("ONE", 0, 256), [[0, 256]], 1)
    iota(R("ZERO", 0, 256), [[0, 256]])
    fill(R("ONEB", 0, 512), 1.0)

    def unit(b):
        o = R("E%d" % b, 0, 512)
        emit("g", lambda: g.affine_select(ap(o), ap(R("ONEB", 0, 512)), [[-1, 512]], A.is_equal, 0.0, b, 4), [o], [R("ONEB", 0, 512)])

    for b in range(4):
        unit(b)

    ts(R("RST", 0, 256), R("JM", 0, 256), 0.0, None, A.not_equal)
    ts(x("SI", 0, 1), x("PI", 0, 1), 15, None, A.bitwise_and)
    cp(x("UL", 0, 8), x("UI", 0, 8))
    cp(x("SP", 0, 1), x("SI", 0, 1))
    s = x("SP", 0, 1)
    ts(R("RMIN", 0, 192), R("RST", 0, 192), 2 * BIG, -BIG, A.mult, A.add)
    ts(R("MASK", 0, 256), R("JM", 0, 256), s, None, A.is_equal)
    fill(R("SEQS", 192, 208), 192.0)
    ts(R("DMASK", 0, 192), R("MASK", 0, 192), 2 * BIG, -BIG, A.mult, A.add)
    fill(R("BIGS", 0, 64), BIG)

    MASK = lambda n: R("MASK", 0, n)
    RST = lambda n: R("RST", 0, n)

    def own(o, n=192):
        return R(o, 15, n, 16)

    act(x("IW"), x("M16"), IDENT, 1.0, s)
    quant("QU", "QUS", "UT", 128)
    quant("QX", "QXS", "XT", 192)
    cp(R("UR", 0, 128, 1, None, dt.uint32), R("QU", 0, 128, 1, R("UL", 0, 8), dt.uint32))
    cp(R("URS", 0, 128), R("QUS", 0, 128, 1, R("UL", 0, 8)))
    mm("PP", "UR", "URS", "QX", "QXS", 192)
    send_codes("UP", "UPS", "UR", "URS", 128, "au")
    act(R("SC", 0, 192), R("PP", 0, 192))
    cp(x("KI"), x("IW"))
    fill(R("XT", 768, 832), 0.0)
    ts(x("KA4"), x("KI"), 2, None, A.arith_shift_right)
    ts(x("KB4"), x("KI"), 3, None, A.bitwise_and)
    ts(x("KI0"), x("KA4"), 3.0, -192.0, A.mult, A.add)
    ts(x("INV"), x("KB4"), 2.5, None, A.is_lt)
    tt(x("ENC"), x("KI0"), x("KB4"), A.add)
    ts(x("H3"), x("IW"), 1.0 / 3, -1.0 / 3, A.mult, A.add)
    tt(x("EN2"), x("ENC"), x("INV"), A.mult)
    tt(x("M17"), x("IW"), x("H3"), A.add)
    ts(x("QVA"), x("EN2"), 192.0, None, A.add)
    tt(R("TMP", 0, 192), R("SC", 0, 192), R("DMASK", 0, 192), A.min)

    def ranks(others=()):
        scan(R("Z", 0, 192), R("RMIN", 0, 192), R("TMP", 0, 192), A.min, A.max, -BIG)
        for c in range(12):
            k = R("Z", 16 * c + 15, 16 * c + 16)
            e = 16 * c + 16
            ts(R("CMP", 192 * c, 192 * c + e), R("SC", 0, e), k, None, A.is_le)
            if e < 192:
                ts(R("CMP", 192 * c + e, 192 * c + 192), R("SC", e, 192), k, None, A.is_lt)
            total(x("CNT", c, c + 1), R("CMP", 192 * c, 192 * c + 192), 192)
            if c < len(others):
                others[c]()
        tt(R("EQR", 0, 192), R("Z", 0, 192), R("SC", 0, 192), A.is_equal)

    def ranks_end():
        tt(x("RK", 0, 12), x("CNT", 0, 12), own("YS"), A.subtract)
        cp(x("RKU", 0, 12), x("RK", 0, 12))

    ranks()
    cp(x("HUA", 0, 12), x("M17", 0, 12))
    scan(R("YS", 0, 192), RST(192), R("EQR", 0, 192))
    ts(x("PHI", 0, 1), x("PI", 0, 1), 4, 1, A.arith_shift_right, A.bitwise_and)
    ts(x("I2", 0, 1), x("SI", 0, 1), 12, None, A.bitwise_and)
    cp(x("PH", 0, 1), x("PHI", 0, 1))
    cp(x("XL", 0, 1), x("I2", 0, 1))
    ts(x("XL", 1, 2), x("I2", 0, 1), 4.0, None, A.add)
    ts(x("AL", 0, 1), x("I2", 0, 1), 3.0, None, A.add)
    ts(x("GM", 0, 32), x("GM", 0, 32), x("PH", 0, 1), None, A.is_equal)
    ranks_end()
    cp(R("SEQS", 0, 192, 1, x("RKU", 0, 12)), R("IOTA", 0, 192))
    tt(R("TMY", 0, 256), R("SEQS", 0, 208, 1, x("QVA")), MASK(256), A.mult)
    scan(R("YS", 0, 256), RST(256), R("TMY", 0, 256))
    for t in range(4):
        ts(R("OFF", 16 * t, 16 * t + 16), own("YS", 256), 4.0, float(t), A.mult, A.add)
    for t in range(4):
        o, a = R("FA", t, W64, 4), R("XT", 0, 784, 1, R("OFF", 16 * t, 16 * t + 16))
        if t < 2:
            act(o, a)
        else:
            cp(o, a)

    F, Fn = "FA", "FB"
    HR, HRn = "HRA", "HRB"
    HU, HUn = "HUA", "HUB"
    QV, QVn = "QVA", "QVB"
    KA, KAn = "KA", "KB"

    def scalar_constants():
        for n in range(4):
            act(R("TP%d" % n, 512, 528), R("ZERO", 0, 16))
        act(x("RST4"), x("C1C"), SIGN)
        act(x("C1C", 16, 32), x("C1C", 16, 32), COPY, 0.25)
        act(x("C1C", 0, 16), x("C1C", 0, 16), IDENT, -0.25, 1.0)
        act(x("C257"), x("IW"), IDENT, -1.0 / BIG, -257.0 / BIG)
        act(x("JW1", 0, 4), x("IW", 0, 4), IDENT, 1.0, 1.0)
        act(x("S16", 0, 1), s, COPY, 1.0 / 16)
        act(x("S161", 0, 1), s, IDENT, 1.0 / 16, 1.0 / 16)
        act(x("D0A", 0, 32), x("PAR", 0, 32), COPY, x("S16", 0, 1))
        act(x("D0B", 0, 32), x("PAR", 0, 32), COPY, x("S161", 0, 1))
        act(x("C64I", 1, 32, 2), x("IW"), IDENT, 1.0, 64.0)
        act(x("HBB", 0, 1), s, IDENT, 12.0 * BIG, 11.5 * BIG)

    keys = [lambda: cp(R("KA", 0, 192, 1, x("RKU", 0, 12)), R("SC", 0, 192))]

    for r in range(ROUNDS):
        last = r == ROUNDS - 1
        qt, qts, lq, ls, lw, lp = ["%s%d" % (n, r) for n in ("QT", "QTS", "LQ", "LS", "LW", "LP")]
        quant("QF", "QFS", F, 256)
        for b in range(4):
            mm("PS%d" % b, "WQ", "WS", "QF", "QFS", 256, 128 * b)
        for b in range(4):
            if b < 2:
                ts(R("G%d" % b, 0, 256), R(F, b, W64, 4), 64.0, None, A.mult)
            else:
                act(R("G%d" % b, 0, 256), R(F, b, W64, 4), COPY, 64.0)
        for b in range(4):
            tt(R("AD%d" % b, 0, 256), R("PS%d" % b, 0, 256), R("G%d" % b, 0, 256), A.add)
            if b < 2:
                act(R("TI", b, W64, 4), R("AD%d" % b, 0, 256), COPY, 0.015625)
        for b in (2, 3):
            ts(R("TI", b, W64, 4), R("AD%d" % b, 0, 256), 0.015625, None, A.mult)

        def plane(b):
            act(R("TP%d" % b, 0, 256), R("AD%d" % b, 0, 256), COPY, 0.015625)

        def unpack(b):
            mm("PD%d" % (b % 2), "EQ%d" % b, "EQS%d" % b, lq, ls)
            act(R("TP%d" % b, 256, 512), R("PD%d" % (b % 2), 0, 256))

        quant(qt, qts, "TI", 256)
        mm("PP", "UR", "URS", qt, qts)
        send_codes(lq, ls, qt, qts, 256, "aq%d" % r)
        keys[0]()
        dma_fold("KW", KA, 192, "fk")
        if r > 0:
            cp(x(HU, 0, 12), x("HW", 0, 12))
        plane(0)
        plane(1)
        act(R("PR", 0, 256), R("PP", 0, 256))
        hu = x(HU, 0, 12)
        tt(R("TMP", 0, 192), R("PR", 0, 256, 1, hu), R("DMASK", 0, 192), A.min)
        act(R("SC", 0, 192), R("PR", 0, 256, 1, hu))
        plane(2)
        plane(3)
        ranks(keys[1:])
        scan(R("YS", 0, 192), RST(192), R("EQR", 0, 192))
        act(R("FLB", 0, 256), R("ZERO", 0, 256))
        if r == 0:
            scalar_constants()
            for b in range(4):
                quant("EQ%d" % b, "EQS%d" % b, "E%d" % b, 128)
        act(R("LBM", 0, 192), R("IOTA", 0, 192), IDENT, -BIG, x("HBB", 0, 1))
        mm("PQ", "UP", "UPS", lq, ls)
        act(R("PPR", 0, 256), R("PQ", 0, 256))
        unpack(0)
        unpack(1)
        ranks_end()
        cp(R("LROW", 0, 192, 1, x("RKU", 0, 12)), R(HR, 0, 192))
        ts(x("LFN", 0, 12), x("RK", 0, 12), 63.5, -BIG, A.is_lt, A.mult)
        tt(R("TMP", 0, 64), R("LROW", 0, 64), MASK(64), A.mult)
        tt(x("LF3", 0, 12), x("LFN", 0, 12), x("C257", 0, 12), A.mult)
        scan(R("LL", 0, 64), RST(64), R("TMP", 0, 64))
        cp(R(lw, 0, 4), own("LL", 64))
        send(R(lp, 0, 4), R(lw, 0, 4), "al%d" % r)
        cp(R("FLB", 0, 256, 1, R(lw, 0, 4)), R("BIGS", 0, 64))
        act(R("SF", 0, 192), R("FLB", 0, 256, 1, hu), IDENT, -1.0 / BIG, 1.0)
        act(R("SFP", 0, 256), R("FLB", 0, 256), IDENT, -1.0 / BIG, 1.0)
        tt(R("KST", 0, 192), R("FLB", 0, 256, 1, hu), R(KA, 0, 192), A.add)
        unpack(2)
        unpack(3)
        tt(R("LBK", 0, 192), R("LBM", 0, 192), R("KST", 0, 192), A.max)
        scan(R("CCS", 0, 192), R("ONE", 0, 192), R("SF", 0, 192))
        red(x("LB", 0, 1), R("LBK", 0, 192), A.min)
        tt(R("XC", 0, 192), R("CCS", 0, 192), R("SF", 0, 192), A.mult)
        dma_fold("XCW", "XC", 192, "fx")
        scan(R("CSP", 0, 256), R("ONE", 0, 256), R("SFP", 0, 256))
        tt(R("TMY", 0, 256), R("XC", 0, 208, 1, x(QV)), MASK(256), A.mult)
        tt(x("CSMB", 1, 17), own("CSP", 256), x("HBP"), A.add)
        scan(R("XWS", 0, 256), RST(256), R("TMY", 0, 256))
        tt(x("NCM"), x("CSMB"), x("CSMB", 1, 17), A.subtract)
        tt(x("KWB", 0, 12), x("KW", 0, 12), x("LFN", 0, 12), A.add)
        if last:
            quant("QVC", "QVS", "VT", 128)
        lpo = R(lp, 0, 4)
        arr = R(KA, 192, 256)
        act(arr, R("PPR", 0, 256, 1, lpo))
        act(x("TH"), x("NCM"), RELU, 1.0, 14.0)
        tt(R("TMP", 0, 64), R("PPR", 0, 256, 1, lpo), MASK(64), A.mult)
        ts(R("ARC", 0, 64), arr, x("LB", 0, 1), None, A.is_lt)
        scan(R("AOS", 0, 64), RST(64), R("TMP", 0, 64))
        red(x("AR1", 0, 1), R("ARC", 0, 64), A.add)

        def cmp_stay(c):
            ts(R("CMN", 192 * c, 192 * c + 192), R("KST", 0, 192), R("AOS", 16 * c + 15, 16 * c + 16), None, A.is_le)
            total(x("TT", 12 + c, 13 + c), R("CMN", 192 * c, 192 * c + 192), 192)

        def cmp_arr(c):
            q = R("CMQ", 64 * c, 64 * c + 64)
            if c >= 12 - ON_SCALAR:
                act(q, arr, RELU, -1.0, x("KWB", c, c + 1))
                total(x("AC0", c, c + 1), q, 64, SIGN)
            else:
                ts(q, arr, x("KWB", c, c + 1), None, A.is_lt)
                total(x("AC0", c, c + 1), q, 64)

        compares = [lambda c=c: cmp_stay(c) for c in range(4)] + [lambda c=c: cmp_arr(c) for c in range(12)]
        sel = R("S4", 0, 16, 1, x("AL", 0, 1))
        tu = x("TU")
        windows = [
            lambda: ts(x("B32", 0, 32), x("GM", 0, 32), x("AR1", 0, 1), None, A.mult),
            lambda: turn(x("B32T", 0, 32), x("B32", 0, 32)),
            lambda: tt(x("ARB", 1, 17), x("B32T", 0, 16), x("B32T", 16, 32), A.add),
            lambda: tt(x("EB", 0, 17), x("ARB", 0, 17), x("CSMB", 0, 17), A.add),
            lambda: tt(x("AX"), x("ARB", 1, 17), x("ARB", 0, 16), A.subtract),
            lambda: tt(x("X2", 0, 32), R("EB", 0, 24, 1, x("XL", 0, 2)), x("C1C", 0, 32), A.mult),
            lambda: tt(x("BA"), x("AX"), x("TH"), A.is_gt),
            lambda: tt(x("CN4", 0, 4), x("EB", 4, 17, 4), x("EB", 0, 13, 4), A.subtract),
            lambda: tt(x("E64"), x("X2", 0, 16), x("X2", 16, 32), A.add),
            lambda: scan(x("S4"), x("RST4"), x("BA"), A.mult, A.max),
            lambda: ts(x("BAD4", 0, 4), x("CN4", 0, 4), 52.5, None, A.is_gt),
            lambda: tt(x("EQD"), x("E64"), x("EB", 0, 16), A.subtract),
            lambda: tt(x("ZX4", 0, 4), x("BAD4", 0, 4), x("S4", 3, 16, 4), A.mult),
            lambda: act(x("XM"), own("XWS", 256), IDENT, 1.0, -193.0),
            lambda: act(x("XV"), own("XWS", 256), SIGN),
            lambda: tt(x("EP1"), sel, x("EQD"), A.mult),
            lambda: tt(x("NI"), sel, x("AX"), A.add),
            lambda: red(x("S256", 0, 1), x("ZX4", 0, 4), A.max),
            lambda: tt(x("EP1"), x("EP1"), x("EB", 0, 16), A.add),
            lambda: ts(x("I0", 1, 32, 2), x("NI"), x("S256", 0, 1), 0.0, A.add, A.is_equal),
            lambda: tt(x("CE3"), x("C12"), x("EP1"), A.subtract),
            lambda: tt(x("ENI"), x("ARB", 0, 16), x("XM"), A.add),
            lambda: ts(x("EP3"), x("CE3"), x("S256", 0, 1), None, A.mult),
            lambda: tt(x("EN2"), x("ENI"), x("XV"), A.mult),
            lambda: tt(x("D1", 1, 33, 2), x("EP1"), x("EP3"), A.add),
            lambda: tt(x("TB", 0, 12), x("XCW", 0, 12), x("LF3", 0, 12), A.add),
            lambda: tt(x("D1", 0, 32, 2), x("D1", 3, 35, 2), x("D1", 1, 33, 2), A.subtract),
            lambda: tt(x("TT", 12, 16), x("JW1", 0, 4), x("TT", 12, 16), A.add),
            lambda: scan(x("UA", 0, 32), x("D0A", 0, 32), x("D1", 0, 32)),
            lambda: scan(x("UB", 0, 32), x("D0B", 0, 32), x("D1", 0, 32)),
            lambda: ts(x("QI"), x("UA", 1, 32, 2), UP_, None, A.add),
            lambda: tt(x("TT", 0, 12), x("TB", 0, 12), x("AC0", 0, 12), A.add),
            lambda: tt(x("VL"), x("UB", 1, 32, 2), x("QI"), A.is_gt),
            lambda: ts(tu, x("TT"), -1.0, None, A.add),
            lambda: tt(x("I1", 1, 32, 2), x("VL"), x("QI"), A.mult),
            lambda: cp(R("SEQ", 0, 448, 1, tu), R(HR, 0, 256)),
            lambda: tt(x("I1", 0, 32, 2), x("EN2"), x("I1", 1, 32, 2), A.subtract),
            lambda: scan(x("UX", 0, 32), x("I0", 0, 32), x("I1", 0, 32)),
            lambda: ts(x(QVn), x("UX", 1, 32, 2), 192.0, None, A.add),
        ]
        act(R(HR, 192, 256), R("IOTA", 256, 512, 1, lpo))
        while compares or windows:
            if windows:
                windows.pop(0)()
            if compares:
                compares.pop(0)()
        if last:
            act(R("HROL", 0, 192), R(HR, 0, 192))
            act(R("HROL", 192, 256), R("IOTA", 256, 320))
        else:
            ts(x("UX", 0, 32, 2), x("UX", 1, 32, 2), 0.0, None, A.is_equal)
        tt(R("TMY", 0, 256), R("SEQ", 0, 208, 1, x(QVn)), MASK(256), A.mult)
        if not last:
            scan(x("UY", 0, 32), x("C64I", 0, 32), x("UX", 0, 32))
        scan(R("YS", 0, 256), RST(256), R("TMY", 0, 256))
        if not last:
            ts(x("QDU"), x("UY", 1, 32, 2), 192.0, None, A.add)
        cp(x("OFY"), own("YS", 256))
        for t in range(3):
            act(R(Fn, t, W64, 4), R("TP%d" % t, 0, 528, 1, x("OFY")))
        if not last:
            cp(R(HRn, 0, 512, 1, x("QDU")), R("IOTA", 0, 256))
            dma_fold("HW", HRn, 192, "fh")
        cp(R(Fn, 3, W64, 4), R("TP3", 0, 528, 1, x("OFY")))
        keys = [
            lambda KA=KA, KAn=KAn: cp(R(KAn, 0, 448, 1, x("TU")), R(KA, 0, 256)),
            lambda: ts(x("HBI"), x("D1", 3, 35, 2), UP_, None, A.add),
            lambda: tt(x("HBP"), x("HBI"), x("C16"), A.subtract),
            lambda: tt(x("M17"), x("HBI"), MASK(16), A.mult),
            lambda: red(x("HB1", 0, 1), x("M17"), A.add),
            lambda: ts(x("HBB", 0, 1), x("HB1", 0, 1), 191.5, BIG, A.add, A.mult),
        ]
        F, Fn, HR, HRn, HU, HUn, QV, QVn, KA, KAn = Fn, F, HRn, HR, HUn, HU, QVn, QV, KAn, KA

    stored = [0]

    def store(q, dst, a, src):
        stored[0] += 1
        emit(q, lambda: Q[q].dma_start(dst, src), [], [a], ("dout", 16 * stored[0], 16))

    cp(R("SEQO", 0, 448, 1, x("TU")), R("HROL", 0, 256))
    quant("QF", "QFS", F, 256)
    mm("PP", "QVC", "QVS", "QF", "QFS")
    cp(R("OLR", 0, 256), R("SEQO", 0, 208, 1, x(QV)))
    act(R("YO", 0, 256), R("PP", 0, 256))
    qf = R("QF", 0, 256, 1, None, dt.uint8)
    store("y", T.oc[:, 0:W64], qf, ap(qf))
    for k in range(4):
        store("y", T.osc[4 * k:4 * k + 4, 0:256], R("QFS", 0, 256), T.QFS[32 * k:32 * k + 4, 0:256])
    store("s", T.y[:, 0:256], R("YO", 0, 256), ap(R("YO", 0, 256)))
    store("y", T.ol[:, 0:256], R("OLR", 0, 256), T.OLR[0:128:16, 0:256])

    for q in ("v", "s", "t", "g"):
        if known["g"].get(q, 0) < cnt[q]:
            g.wait_ge(T.sem[sem_of[q]], cnt[q])
    for n in ("dx", "du", "dw", "dws", "dv"):
        g.wait_ge(T.sem[n], 16)
    for n in ("fk", "fx", "fh"):
        g.wait_ge(T.sem[n], folded[n])
    g.wait_ge(T.sem["dout"], 16 * stored[0])
    g.wait_ge(T.sem["loc"], sent[0])
    g.wait_ge(T.sem["au"], 2 * engines)
    for r in range(ROUNDS):
        g.wait_ge(T.sem["aq%d" % r], 2 * engines)
        g.wait_ge(T.sem["al%d" % r], engines)
